import numpy as np
import ml_dtypes


def mxq(x, axis, fmt="e4m3"):
    dtype, down = {"e4m3": (ml_dtypes.float8_e4m3fn, 7), "e5m2": (ml_dtypes.float8_e5m2, 14)}[fmt]
    v = np.moveaxis(np.asarray(x, np.float32).astype(ml_dtypes.bfloat16).astype(np.float64), axis, -1)
    blocks = v.reshape(v.shape[:-1] + (-1, 32))
    amax = np.abs(blocks).max(-1, keepdims=True)
    byte = np.maximum(np.where(amax > 0, np.frexp(amax)[1] - 1 + 127, 0) - down, 1)
    scale = np.exp2(byte - 127.0)
    codes = (blocks / scale).astype(np.float32).astype(dtype).astype(np.float64)
    return np.moveaxis((codes * scale).reshape(v.shape), -1, axis)


WIDE = False


def mx_kscale(k):
    if not WIDE:
        return np.ones(k)
    levels = np.array([10, -10, 5, -5, 0])
    if k % 512:
        return np.exp2(np.random.permutation(np.resize(levels, k // 32))).repeat(32)
    a = np.empty((k // 512, 16))
    for p in range(k // 512):
        a[p, :8] = np.random.permutation(np.resize(levels, 8))
        for g in range(8):
            far = levels[np.abs(levels - a[p, g]) >= 10]
            a[p, g + 8] = far[np.random.randint(len(far))]
    return np.exp2(a.ravel()).repeat(32)


BF16 = ml_dtypes.bfloat16


def bf(x):
    return np.asarray(x, np.float32).astype(BF16)


def f64(x):
    return np.asarray(x).astype(np.float64)


T, D, E, R, F = 4096, 1024, 2, 512, 128


def expert_scores(a):
    return np.sqrt(np.sum(a * a, axis=-1))


def silu(v):
    return v / (1.0 + np.exp(-v))


def softmax_experts(score):
    e = np.exp(score - score.max(axis=0, keepdims=True))
    return e / e.sum(axis=0, keepdims=True)


def draw0():
    s, t = mx_kscale(D), mx_kscale(R)
    return {"x": bf(np.random.standard_normal((T, D)) * s),
            "wdown": bf(np.random.standard_normal((E, D, R)) / np.sqrt(D) / s[None, :, None]),
            "rgain": bf((1.0 + 0.1 * np.random.standard_normal((E, R))) * t),
            "wup": bf(np.random.standard_normal((E, R, F)) * 1.5 / np.sqrt(R) / t[None, :, None]),
            "wp": bf(np.random.standard_normal((E, D, F)) / np.sqrt(D) / s[None, :, None])}


def core(x, wdown, rgain, wup, wp):
    xq = mxq(f64(x), 1, "e4m3")
    a = xq @ mxq(f64(wdown), 1, "e4m3")
    score = expert_scores(a)
    g = softmax_experts(score)
    b = a * f64(rgain)[:, None, :]
    u = mxq(b, 2, "e4m3") @ mxq(f64(wup), 1, "e4m3")
    p = xq @ mxq(f64(wp), 1, "e4m3")
    return np.sum(g[:, :, None] * silu(u) * p, axis=0)


def e4m3fn_bytes(y):
    return np.clip(np.asarray(y, np.float64), -448.0, 448.0).astype(np.float32).astype(ml_dtypes.float8_e4m3fn).view(np.uint8)


def e4m3fn_values(b):
    return np.asarray(b, np.uint8).view(ml_dtypes.float8_e4m3fn).astype(np.float64)


def setup_inputs():
    d = draw0()
    x0 = np.asarray(d['x']).astype(np.float64)
    s = (np.max(np.abs(x0), axis=(0,), keepdims=True) / 448.0).astype(np.float32)
    out = {}
    for k, v in d.items():
        if k == 'x':
            out['x_bytes'] = e4m3fn_bytes(x0 / s.astype(np.float64))
            out['x_scale'] = s
        else:
            out[k] = v
    return out


def reference(x_bytes, x_scale, wdown, rgain, wup, wp):
    return core(e4m3fn_values(x_bytes) * x_scale.astype(np.float64), wdown, rgain, wup, wp)

@@ -1,0 +1,453 @@
+from contextlib import ExitStack
+
+import concourse.mybir as mybir
+from concourse.masks import make_identity
+
+T, D, E, R, F = 4096, 1024, 2, 512, 128
+P = 128
+PAIRS = T // (2 * P)
+TILES = 2 * PAIRS
+FLOPS = 2 * T * (D * E * R + D * E * F + E * R * F)
+
+F32 = mybir.dt.float32
+BF16 = mybir.dt.bfloat16
+I32 = mybir.dt.int32
+U32 = mybir.dt.uint32
+U8 = mybir.dt.uint8
+F8 = mybir.dt.float8_e4m3fn
+X4 = mybir.dt.float8_e4m3fn_x4
+ACT = mybir.ActivationFunctionType
+ALU = mybir.AluOpType
+
+SQRT_SEED = 532487669.0
+GROUPS = (7, 4, 3, 2)
+AHEAD = 9
+PACE = 1.0
+FLAG = 20
+FEND = 73
+WENG = 'vssssvss'
+WPER = 2
+WFROM = 2
+WLAG = 2
+TURN = ('xt', 2, 'xt', 2)
+SEED = 0
+LATE = 0
+LS = 11
+SINGLES = 16
+LTX, LLX, LTB, LLB, LMA, LQX, LQB = 7, 6, 2, 3, 1, 4, 5
+STEP = ('SI', 'S1', 'WQ', 'SX', 'QW', 'S0', 'LX', 'AD', 'QX', 'M1', 'M0', 'LB', 'ZS', 'N', 'MF', 'N', 'QB', 'W', 'MX', 'TX', 'TB', 'G1', 'N', 'G0', 'LA')
+LATEST = ('MF', 'M0', 'WQ', 'S0', 'M1', 'S1', 'W', 'AD', 'N', 'LX', 'LA', 'G0', 'SI', 'ZS', 'QW', 'N', 'TX', 'MX', 'G1', 'TB', 'QX', 'N', 'SX', 'QB', 'LB')
+TAIL = ('N', 'LA', 'QB', 'MF', 'N', 'SI', 'ZS', 'LB', 'MX', 'N', 'AD', 'TB', 'N')
+
+
+def tile_autonomyofexpertsnormgate_t_kernel(tc, x_bytes, x_scale, wdown, rgain, wup, wp, out):
+    nc = tc.nc
+    with ExitStack() as ctx:
+        keep = ctx.enter_context(tc.tile_pool(name="keep", bufs=1))
+        stage = ctx.enter_context(tc.tile_pool(name="stage", bufs=2))
+        psum = ctx.enter_context(tc.psum_pool(name="psum", bufs=1))
+        ctx.enter_context(tc.manual_schedule())
+
+        xscale = keep.tile([P, 2, D], F32, name="xscale")
+        tiny = keep.tile([P, 1], F32, name="tiny")
+        nc.vector.memset(tiny[:], 0.0)
+        gain = keep.tile([P, E, 2 * P, 2], BF16, name="gain")
+
+        xb = {}
+
+        def load_x(k):
+            xb_tile = stage.tile([P, 2, D], U8, name="xb", bufs=6)
+            xb[k] = xb_tile
+            nc.sync.dma_start(out=xb[k][:], in_=x_bytes[256 * k : 256 * k + 256, :].rearrange("(p m) d -> p m d", m=2))
+
+        wraw, wcode, wscale = {}, {}, {}
+
+        def load_w(e, g):
+            w_tile = keep.tile([P, 4, R], BF16, name="wraw%d%d" % (e, g))
+            wraw[e, g] = w_tile
+            nc.sync.dma_start(out=w_tile[:], in_=wdown[e, 512 * g : 512 * g + 512, :].rearrange("(p j) c -> p j c", j=4))
+
+        first = stage.tile([P, 2, D], U8, name="xb", bufs=6)
+        xb[0] = first
+        tokens = x_bytes[0:256, :].rearrange("(p m) d -> p m d", m=2)
+        spread = x_scale.rearrange("o k -> (o k)")
+        nc.sync.dma_start(out=xscale[:, 0, 0:512], in_=spread[0:512].partition_broadcast(P))
+        nc.sync.dma_start(out=first[:, 0, :], in_=tokens[:, 0, :])
+        nc.sync.dma_start(out=xscale[:, 0, 512:1024], in_=spread[512:1024].partition_broadcast(P))
+        nc.sync.dma_start(out=first[:, 1, :], in_=tokens[:, 1, :])
+        nc.scalar.activation(out=tiny[:], in_=tiny[:], func=ACT.Silu)
+        nc.scalar.copy(out=xscale[:, 1, :], in_=xscale[:, 0, :])
+        load_w(0, 0)
+        load_x(1)
+        load_w(0, 1)
+        load_w(1, 0)
+        load_x(2)
+        load_w(1, 1)
+        nc.scalar.dma_start(out=gain[:].rearrange("q e a i -> q (e a i)"), in_=rgain.rearrange("e r -> (e r)").partition_broadcast(P))
+        load_x(3)
+        praw = keep.tile([P, E, 2, 4, F], BF16, name="praw")
+        for e in range(E):
+            nc.sync.dma_start(out=praw[:, e], in_=wp[e].rearrange("(g p j) f -> p g j f", g=2, j=4))
+        uraw = keep.tile([P, E, 4, F], BF16, name="uraw")
+        nc.sync.dma_start(out=uraw[:], in_=wup.rearrange("e (p j) f -> p e j f", j=4))
+        for k in range(4, PAIRS):
+            load_x(k)
+
+        ident = keep.tile([P, P], F32, name="ident")
+        make_identity(nc, ident[:])
+
+        wgrp = {}
+
+        def group_w(eng, e, g, u):
+            if u == 0:
+                wg_tile = stage.tile([P, 4 * R], BF16, align_bytes=64, name="wgrp", bufs=2)
+                wgrp[e, g] = wg_tile
+            half = wgrp[e, g][:, 1024 * u : 1024 * (u + 1)].rearrange("q (i p j) -> q i p j", i=2, j=4)
+            src = wraw[e, g][:].rearrange("q j (p t) -> q t p j", t=4)[:, 2 * u : 2 * u + 2]
+            if eng == "s":
+                nc.scalar.copy(out=half, in_=src)
+            elif eng == "g":
+                nc.gpsimd.tensor_copy(out=half, in_=src)
+            else:
+                nc.vector.tensor_copy(out=half, in_=src)
+
+        def quant_w(e, g):
+            c_tile = keep.tile([P, R], U32, align_bytes=64, name="wcode%d%d" % (e, g))
+            s_tile = keep.tile([P, R], U8, align_bytes=64, name="wscale%d%d" % (e, g))
+            wcode[e, g], wscale[e, g] = c_tile, s_tile
+            nc.vector.quantize_mx(out=c_tile[:].bitcast(X4), scales=s_tile[:], in_=wgrp[e, g][:])
+
+        pgrp = keep.tile([P, 2, 4 * E * F], BF16, align_bytes=64, name="pgrp")
+        pcode = keep.tile([P, 2, E * F], U32, align_bytes=64, name="pcode")
+        pscale = keep.tile([P, 2, E * F], U8, align_bytes=64, name="pscale")
+        ugrp = keep.tile([P, 4 * E * F], BF16, align_bytes=64, name="ugrp")
+        ucode = keep.tile([P, E * F], U32, align_bytes=64, name="ucode")
+        uscale = keep.tile([P, E * F], U8, align_bytes=64, name="uscale")
+
+        def group_p(g):
+            nc.scalar.copy(
+                out=pgrp[:, g, :].rearrange("q (e f j) -> q e f j", e=E, j=4),
+                in_=praw[:, :, g].rearrange("q e j f -> q e f j"),
+            )
+
+        def quant_p(g):
+            nc.vector.quantize_mx(out=pcode[:, g, :].bitcast(X4), scales=pscale[:, g, :], in_=pgrp[:, g, :])
+
+        def group_u():
+            nc.scalar.copy(
+                out=ugrp[:].rearrange("q (e f j) -> q e f j", e=E, j=4),
+                in_=uraw[:].rearrange("q e j f -> q e f j"),
+            )
+
+        def quant_u():
+            nc.vector.quantize_mx(out=ucode[:].bitcast(X4), scales=uscale[:], in_=ugrp[:])
+
+        sums = []
+        clock = [0]
+        late = []
+
+        xs, xt, xg, xc, xsc = {}, {}, {}, {}, {}
+        acc, bb, bt, bg, bc, bsc = {}, {}, {}, {}, {}, {}
+        ACCS = 8 - 2 - TURN[1] - (TURN[3] if TURN[0] != TURN[2] else 0)
+        pps, ups, sil, q, z = {}, {}, {}, {}, {}
+        sumsq = keep.tile([P, TILES * E], F32, name="sumsq")
+        gate = keep.tile([P, TILES, E], F32, name="gate")
+
+        def scale_x(n):
+            k, m = n // 2, n % 2
+            if m == 0:
+                xs_tile = stage.tile([P, 2, D], BF16, align_bytes=64, name="xs", bufs=AHEAD // 2 + 2)
+                xs[k] = xs_tile
+            if n == 0:
+                for c in range(2):
+                    cols = slice(512 * c, 512 * (c + 1))
+                    nc.vector.tensor_tensor(out=xs[k][:, 0, cols], in0=xb[k][:, 0, cols].bitcast(F8), in1=xscale[:, 0, cols], op=ALU.mult)
+                return 1
+            if k < SINGLES:
+                nc.vector.tensor_tensor(out=xs[k][:, m, :], in0=xb[k][:, m, :].bitcast(F8), in1=xscale[:, 0, :], op=ALU.mult)
+                return 1
+            nc.vector.tensor_tensor(
+                out=xs[k][:].rearrange("q m d -> q (m d)"),
+                in0=xb[k][:].rearrange("q m d -> q (m d)").bitcast(F8),
+                in1=xscale[:].rearrange("q m d -> q (m d)"),
+                op=ALU.mult,
+            )
+            return 2
+
+        def turn_x(n):
+            xt_tile = psum.tile([P, 2, 2, P], F32, name=TURN[0], bufs=TURN[1])
+            xt[n] = xt_tile
+            words = xs[n // 2][:, n % 2, :].bitcast(F32)
+            for g in range(2):
+                for u in range(2):
+                    nc.tensor.transpose(xt_tile[:, g, u, :], words[:, 256 * g + u : 256 * (g + 1) : 2], ident[:])
+
+        def leave_x(n):
+            k, m = n // 2, n % 2
+            if m == 0:
+                xg_tile = stage.tile([P, 2 * D], BF16, align_bytes=64, name="xg", bufs=3)
+                xg[k] = xg_tile
+            nc.scalar.copy(
+                out=xg[k][:, D * m : D * (m + 1)].bitcast(F32).rearrange("q (g r u) -> q g r u", g=2, u=2),
+                in_=xt[n][:].rearrange("q g u r -> q g r u"),
+            )
+
+        def quant_x(k):
+            c_tile = keep.tile([P, 4 * P], U32, align_bytes=64, name="xc%d" % k)
+            s_tile = keep.tile([P, 4 * P], U8, align_bytes=64, name="xsc%d" % k)
+            xc[k], xsc[k] = c_tile, s_tile
+            nc.vector.quantize_mx(out=c_tile[:].bitcast(X4), scales=s_tile[:], in_=xg[k][:])
+
+        def mm_a(n, e):
+            k, m = n // 2, n % 2
+            a_tile = psum.tile([P, R], F32, name="acc", bufs=ACCS)
+            acc[n, e] = a_tile
+            for g in range(2):
+                cols = slice((2 * m + g) * P, (2 * m + g + 1) * P)
+                nc.tensor.matmul_mx(
+                    out=a_tile[:],
+                    lhsT=xc[k][:, cols].bitcast(X4),
+                    lhsT_scale=xsc[k][:, cols],
+                    rhs=wcode[e, g][:].bitcast(X4),
+                    rhs_scale=wscale[e, g][:],
+                    start=(g == 0),
+                    stop=(g == 1),
+                )
+
+        def gain_b(n, e):
+            if n not in bb:
+                bb_tile = stage.tile([P, E * R], BF16, align_bytes=64, name="bb", bufs=3)
+                bb[n] = bb_tile
+            nc.vector.tensor_tensor(
+                out=bb[n][:, e * R : (e + 1) * R].rearrange("q (u p i) -> q u p i", u=2, i=2),
+                in0=acc[n, e][:].rearrange("q (u i p) -> q u p i", u=2, i=2),
+                in1=gain[:, e].rearrange("q (p u) i -> q u p i", u=2),
+                op=ALU.mult,
+            )
+
+        def new_bg(k):
+            if k not in bg:
+                bg_tile = stage.tile([P, 2 * E * R], BF16, align_bytes=64, name="bg", bufs=3)
+                bg[k] = bg_tile
+
+        def square(n, e):
+            junk = stage.tile([P, R], BF16, name="junk", bufs=2)
+            nc.scalar.activation(out=junk[:], in_=acc[n, e][:], func=ACT.Square, accum_out=sumsq[:, 2 * n + e : 2 * n + e + 1])
+
+        def turn_b(n):
+            bt_tile = psum.tile([P, E, 2, P], F32, name=TURN[2], bufs=TURN[3])
+            bt[n] = bt_tile
+            words = bb[n][:].bitcast(F32)
+            for e in range(E):
+                for u in range(2):
+                    nc.tensor.transpose(bt_tile[:, e, u, :], words[:, 256 * e + 128 * u : 256 * e + 128 * (u + 1)], ident[:])
+
+        def leave_b(n):
+            k, m = n // 2, n % 2
+            ne = E
+            new_bg(k)
+            nc.scalar.copy(
+                out=bg[k][:, E * R * m : E * R * m + ne * R].bitcast(F32).rearrange("q (e r u) -> q e r u", e=ne, u=2),
+                in_=bt[n][:, 0:ne].rearrange("q e u r -> q e r u"),
+            )
+
+        def quant_b(k):
+            c_tile = keep.tile([P, 4 * P], U32, align_bytes=64, name="bc%d" % k)
+            s_tile = keep.tile([P, 4 * P], U8, align_bytes=64, name="bsc%d" % k)
+            bc[k], bsc[k] = c_tile, s_tile
+            nc.vector.quantize_mx(out=c_tile[:].bitcast(X4), scales=s_tile[:], in_=bg[k][:])
+
+        def mm_final(k):
+            p_tile = psum.tile([P, 2, E * F], F32, name="pp")
+            u_tile = psum.tile([P, 2, E, F], F32, name="uu")
+            pps[k], ups[k] = p_tile, u_tile
+            for m in range(2):
+                for e in range(E):
+                    cols = slice((2 * m + e) * P, (2 * m + e + 1) * P)
+                    ecols = slice(e * F, (e + 1) * F)
+                    nc.tensor.matmul_mx(
+                        out=u_tile[:, m, e, :],
+                        lhsT=bc[k][:, cols].bitcast(X4),
+                        lhsT_scale=bsc[k][:, cols],
+                        rhs=ucode[:, ecols].bitcast(X4),
+                        rhs_scale=uscale[:, ecols],
+                        start=True,
+                        stop=True,
+                    )
+            for m in range(2):
+                for g in range(2):
+                    cols = slice((2 * m + g) * P, (2 * m + g + 1) * P)
+                    nc.tensor.matmul_mx(
+                        out=p_tile[:, m, :],
+                        lhsT=xc[k][:, cols].bitcast(X4),
+                        lhsT_scale=xsc[k][:, cols],
+                        rhs=pcode[:, g, :].bitcast(X4),
+                        rhs_scale=pscale[:, g, :],
+                        start=(g == 0),
+                        stop=(g == 1),
+                    )
+
+        def silu(k):
+            s_tile = stage.tile([P, 2, E, F], F32, name="sil", bufs=2)
+            sil[k] = s_tile
+            nc.scalar.activation(out=s_tile[:], in_=ups[k][:], func=ACT.Silu)
+
+        def mix(k):
+            q_tile = stage.tile([P, 2, E, F], F32, name="q", bufs=3)
+            q[k] = q_tile
+            nc.vector.tensor_tensor(
+                out=q_tile[:].rearrange("q m e f -> q (m e f)"),
+                in0=sil[k][:].rearrange("q m e f -> q (m e f)"),
+                in1=pps[k][:].rearrange("q m f -> q (m f)"),
+                op=ALU.mult,
+            )
+
+        def weigh(k):
+            z_tile = stage.tile([P, 2, F], F32, name="z", bufs=3)
+            z[k] = z_tile
+            for m in range(2):
+                nc.scalar.activation(out=z_tile[:, m, :], in_=q[k][:, m, 1, :], func=ACT.Copy, scale=gate[:, 2 * k + m, 1:2])
+
+        def join(k):
+            o = stage.tile([P, 2, F], F32, name="o", bufs=3)
+            for m in range(2):
+                nc.vector.scalar_tensor_tensor(
+                    out=o[:, m, :], in0=q[k][:, m, 0, :], scalar=gate[:, 2 * k + m, 0:1], in1=z[k][:, m, :], op0=ALU.mult, op1=ALU.add
+                )
+            nc.sync.dma_start(out=out[256 * k : 256 * k + 256, :].rearrange("(p m) f -> p m f", m=2), in_=o[:])
+
+        def gate_steps(first, count):
+            t0, nt = 2 * first, 2 * count
+            ss = sumsq[:, E * t0 : E * (t0 + nt)]
+            seed = stage.tile([P, E * nt], I32, name="seed", bufs=2)
+            state = {"y": seed[:].bitcast(F32)}
+
+            def start():
+                nc.vector.tensor_scalar(out=seed[:], in0=ss.bitcast(I32), scalar1=0.5, scalar2=SQRT_SEED, op0=ALU.mult, op1=ALU.add)
+
+            def recip():
+                r = stage.tile([P, E * nt], F32, name="newton_r", bufs=2)
+                state["r"] = r
+                nc.vector.reciprocal(out=r[:], in_=state["y"])
+
+            def divide():
+                t = stage.tile([P, E * nt], F32, name="newton_t", bufs=2)
+                state["t"] = t
+                nc.vector.scalar_tensor_tensor(out=t[:], in0=ss, scalar=0.5, in1=state["r"][:], op0=ALU.mult, op1=ALU.mult)
+
+            def average():
+                y = stage.tile([P, E * nt], F32, name="newton_y", bufs=2)
+                nc.vector.scalar_tensor_tensor(out=y[:], in0=state["y"], scalar=0.5, in1=state["t"][:], op0=ALU.mult, op1=ALU.add)
+                state["y"] = y[:]
+
+            def finish():
+                d = stage.tile([P, nt], F32, name="gate_d", bufs=2)
+                h = stage.tile([P, nt], F32, name="gate_h", bufs=2)
+                both = state["y"].rearrange("q (n e) -> q e n", e=E)
+                nc.vector.tensor_tensor(out=d[:], in0=both[:, 0], in1=both[:, 1], op=ALU.subtract)
+                late.append((clock[0] + LATE, lambda: squash(d, h)))
+
+            def squash(d, h):
+                nc.scalar.activation(out=h[:], in_=d[:], func=ACT.Tanh, scale=0.5)
+                for e in range(E):
+                    nc.scalar.activation(out=gate[:, t0 : t0 + nt, e], in_=h[:], func=ACT.Copy, scale=(0.5, -0.5)[e], bias=0.5)
+                ready.extend(range(first, first + count))
+
+            return [start] + [recip, divide, average] * 3 + [finish]
+
+        silus = []
+        scales = []
+        small = []
+        ready = []
+        final = []
+        bounds, total = {}, 0
+        for count in GROUPS:
+            bounds[2 * (total + count) - 1] = (total, count)
+            total += count
+
+        def weave(count):
+            for i in range(count):
+                if small:
+                    small.pop(0)()
+
+        done = 0
+        s = -AHEAD
+        waiting = []
+        scaled = 0
+        while done < PAIRS:
+            clock[0] = s
+            busy = 0 <= s < TILES
+            for tok in (TAIL if s >= TILES else LATEST if s >= LS else STEP):
+                if tok == "TX" and 0 <= s + LTX < TILES:
+                    turn_x(s + LTX)
+                elif tok == "LX" and 0 <= s + LLX < TILES:
+                    leave_x(s + LLX)
+                elif tok == "TB" and 0 <= s - LTB < TILES:
+                    turn_b(s - LTB)
+                elif tok == "LB" and 0 <= s - LLB < TILES:
+                    leave_b(s - LLB)
+                elif tok == "G0" and busy:
+                    gain_b(s, 0)
+                elif tok == "G1" and busy:
+                    gain_b(s, 1)
+                elif tok == "S0" and busy:
+                    square(s, 0)
+                elif tok == "S1" and busy:
+                    square(s, 1)
+                elif tok == "M0" and 0 <= s + LMA < TILES:
+                    mm_a(s + LMA, 0)
+                elif tok == "M1" and 0 <= s + LMA < TILES:
+                    mm_a(s + LMA, 1)
+                elif tok == "SX" and scaled < TILES and (scaled - AHEAD <= s if s < 0 else (scaled - AHEAD) * PACE <= s):
+                    scaled += scale_x(scaled)
+                elif tok == "N":
+                    weave(1)
+                elif tok == "MX" and final:
+                    mix(final[0])
+                    scales.append(final[0])
+                    sums.append(final.pop(0))
+                    done += 1
+                elif tok == "ZS" and scales:
+                    weigh(scales.pop(0))
+                elif tok == "AD" and sums and sums[0] not in scales:
+                    join(sums.pop(0))
+                elif tok == "LA" and late and (s >= late[0][0] or s >= TILES):
+                    late.pop(0)[1]()
+                elif tok == "QX" and (s + LQX) % 2 == 0 and 0 <= (s + LQX) // 2 < PAIRS:
+                    quant_x((s + LQX) // 2)
+                elif tok == "QB" and (s - LQB) % 2 == 0 and 0 <= (s - LQB) // 2 < PAIRS:
+                    quant_b((s - LQB) // 2)
+                elif tok == "W":
+                    for w in range(WPER * (s + AHEAD - WFROM), WPER * (s + AHEAD - WFROM + 1)):
+                        if 0 <= w < 8:
+                            group_w(WENG[w], w // 4, w // 2 % 2, w % 2)
+                elif tok == "WQ":
+                    for w in range(WPER * (s + AHEAD - WFROM - WLAG), WPER * (s + AHEAD - WFROM - WLAG + 1)):
+                        if 0 <= w < 8 and w % 2 == 1:
+                            quant_w(w // 4, w // 2 % 2)
+                    if s in (1, 2):
+                        group_p(s - 1)
+                    if s == 3:
+                        group_u()
+                elif tok == "QW":
+                    if s in (4, 5):
+                        quant_p(s - 4)
+                    if s == 6:
+                        quant_u()
+                elif tok == "MF":
+                    if ready and ready[0] in bc and not final and (s >= 2 * ready[0] + FLAG or s >= TILES - FEND):
+                        k = ready.pop(0)
+                        mm_final(k)
+                        final.append(k)
+                        silus.append(k)
+                elif tok == "SI" and silus:
+                    silu(silus.pop(0))
+            if s in bounds:
+                waiting.append((s + SEED, bounds[s]))
+            if waiting and waiting[0][0] <= s:
+                small.extend(gate_steps(*waiting.pop(0)[1]))
+            s += 1
+        while scales:
+            weigh(scales.pop(0))
+        while sums:
+            join(sums.pop(0))

@@ -5,8 +5,8 @@ from concourse.masks import make_identity
 
 T, D, E, R, F = 4096, 1024, 2, 512, 128
 P = 128
-PAIRS = T // (2 * P)
-TILES = 2 * PAIRS
+TILES = T // P
+PAIRS = TILES // 2
 FLOPS = 2 * T * (D * E * R + D * E * F + E * R * F)
 
 F32 = mybir.dt.float32
@@ -20,24 +20,12 @@ ACT = mybir.ActivationFunctionType
 ALU = mybir.AluOpType
 
 SQRT_SEED = 532487669.0
-GROUPS = (7, 4, 3, 2)
-AHEAD = 9
-PACE = 1.0
-FLAG = 20
-FEND = 73
-WENG = 'vssssvss'
-WPER = 2
-WFROM = 2
-WLAG = 2
-TURN = ('xt', 2, 'xt', 2)
-SEED = 0
-LATE = 0
-LS = 11
-SINGLES = 16
-LTX, LLX, LTB, LLB, LMA, LQX, LQB = 7, 6, 2, 3, 1, 4, 5
-STEP = ('SI', 'S1', 'WQ', 'SX', 'QW', 'S0', 'LX', 'AD', 'QX', 'M1', 'M0', 'LB', 'ZS', 'N', 'MF', 'N', 'QB', 'W', 'MX', 'TX', 'TB', 'G1', 'N', 'G0', 'LA')
-LATEST = ('MF', 'M0', 'WQ', 'S0', 'M1', 'S1', 'W', 'AD', 'N', 'LX', 'LA', 'G0', 'SI', 'ZS', 'QW', 'N', 'TX', 'MX', 'G1', 'TB', 'QX', 'N', 'SX', 'QB', 'LB')
-TAIL = ('N', 'LA', 'QB', 'MF', 'N', 'SI', 'ZS', 'LB', 'MX', 'N', 'AD', 'TB', 'N')
+GROUPS = (6, 6, 4)
+TURN_AHEAD = 6
+HEAD_TILES = 12
+DOUBLE_STEPS = 2
+WEIGHT_ENGINES = "ssss"
+JOINS = 4
 
 
 def tile_autonomyofexpertsnormgate_t_kernel(tc, x_bytes, x_scale, wdown, rgain, wup, wp, out):
@@ -48,164 +36,132 @@ def tile_autonomyofexpertsnormgate_t_kernel(tc, x_bytes, x_scale, wdown, rgain, 
         psum = ctx.enter_context(tc.psum_pool(name="psum", bufs=1))
         ctx.enter_context(tc.manual_schedule())
 
-        xscale = keep.tile([P, 2, D], F32, name="xscale")
-        tiny = keep.tile([P, 1], F32, name="tiny")
-        nc.vector.memset(tiny[:], 0.0)
-        gain = keep.tile([P, E, 2 * P, 2], BF16, name="gain")
-
-        xb = {}
+        xscale = keep.tile([P, D], F32, name="xscale")
+        xb, wraw = {}, {}
 
         def load_x(k):
-            xb_tile = stage.tile([P, 2, D], U8, name="xb", bufs=6)
-            xb[k] = xb_tile
+            xb[k] = keep.tile([P, 2, D], U8, name="xb%d" % k)
             nc.sync.dma_start(out=xb[k][:], in_=x_bytes[256 * k : 256 * k + 256, :].rearrange("(p m) d -> p m d", m=2))
 
-        wraw, wcode, wscale = {}, {}, {}
-
         def load_w(e, g):
-            w_tile = keep.tile([P, 4, R], BF16, name="wraw%d%d" % (e, g))
-            wraw[e, g] = w_tile
-            nc.sync.dma_start(out=w_tile[:], in_=wdown[e, 512 * g : 512 * g + 512, :].rearrange("(p j) c -> p j c", j=4))
+            wraw[e, g] = keep.tile([P, 4, R], BF16, name="wraw%d%d" % (e, g))
+            nc.sync.dma_start(out=wraw[e, g][:], in_=wdown[e, 512 * g : 512 * g + 512, :].rearrange("(p j) c -> p j c", j=4))
 
-        first = stage.tile([P, 2, D], U8, name="xb", bufs=6)
-        xb[0] = first
-        tokens = x_bytes[0:256, :].rearrange("(p m) d -> p m d", m=2)
         spread = x_scale.rearrange("o k -> (o k)")
-        nc.sync.dma_start(out=xscale[:, 0, 0:512], in_=spread[0:512].partition_broadcast(P))
-        nc.sync.dma_start(out=first[:, 0, :], in_=tokens[:, 0, :])
-        nc.sync.dma_start(out=xscale[:, 0, 512:1024], in_=spread[512:1024].partition_broadcast(P))
-        nc.sync.dma_start(out=first[:, 1, :], in_=tokens[:, 1, :])
-        nc.scalar.activation(out=tiny[:], in_=tiny[:], func=ACT.Silu)
-        nc.scalar.copy(out=xscale[:, 1, :], in_=xscale[:, 0, :])
+        xb[0] = keep.tile([P, 2, D], U8, name="xb0")
+        for half in range(2):
+            cols = slice(512 * half, 512 * half + 512)
+            nc.sync.dma_start(out=xscale[:, cols], in_=spread[cols].partition_broadcast(P))
+            nc.sync.dma_start(out=xb[0][:, half, :], in_=x_bytes[0:256, :].rearrange("(p m) d -> p m d", m=2)[:, half, :])
         load_w(0, 0)
         load_x(1)
         load_w(0, 1)
         load_w(1, 0)
         load_x(2)
         load_w(1, 1)
-        nc.scalar.dma_start(out=gain[:].rearrange("q e a i -> q (e a i)"), in_=rgain.rearrange("e r -> (e r)").partition_broadcast(P))
+        graw = keep.tile([P, E * R], BF16, name="graw")
+        nc.sync.dma_start(out=graw[:], in_=rgain.rearrange("e r -> (e r)").partition_broadcast(P))
         load_x(3)
+        load_x(4)
         praw = keep.tile([P, E, 2, 4, F], BF16, name="praw")
         for e in range(E):
             nc.sync.dma_start(out=praw[:, e], in_=wp[e].rearrange("(g p j) f -> p g j f", g=2, j=4))
         uraw = keep.tile([P, E, 4, F], BF16, name="uraw")
         nc.sync.dma_start(out=uraw[:], in_=wup.rearrange("e (p j) f -> p e j f", j=4))
-        for k in range(4, PAIRS):
+        for k in range(5, PAIRS):
             load_x(k)
 
         ident = keep.tile([P, P], F32, name="ident")
         make_identity(nc, ident[:])
 
-        wgrp = {}
+        wgrp, wcode, wscale = {}, {}, {}
 
-        def group_w(eng, e, g, u):
-            if u == 0:
-                wg_tile = stage.tile([P, 4 * R], BF16, align_bytes=64, name="wgrp", bufs=2)
-                wgrp[e, g] = wg_tile
-            half = wgrp[e, g][:, 1024 * u : 1024 * (u + 1)].rearrange("q (i p j) -> q i p j", i=2, j=4)
-            src = wraw[e, g][:].rearrange("q j (p t) -> q t p j", t=4)[:, 2 * u : 2 * u + 2]
-            if eng == "s":
-                nc.scalar.copy(out=half, in_=src)
-            elif eng == "g":
-                nc.gpsimd.tensor_copy(out=half, in_=src)
+        def group_w(e, g):
+            wgrp[e, g] = stage.tile([P, 4 * R], BF16, align_bytes=64, name="wgrp", bufs=2)
+            dst = wgrp[e, g][:].rearrange("q (u p i j) -> q p j u i", u=2, i=2, j=4)
+            src = wraw[e, g][:].rearrange("q j (p u i) -> q p j u i", u=2, i=2)
+            if WEIGHT_ENGINES[2 * e + g] == "s":
+                nc.scalar.copy(out=dst, in_=src)
             else:
-                nc.vector.tensor_copy(out=half, in_=src)
+                nc.vector.tensor_copy(out=dst, in_=src)
 
         def quant_w(e, g):
-            c_tile = keep.tile([P, R], U32, align_bytes=64, name="wcode%d%d" % (e, g))
-            s_tile = keep.tile([P, R], U8, align_bytes=64, name="wscale%d%d" % (e, g))
-            wcode[e, g], wscale[e, g] = c_tile, s_tile
-            nc.vector.quantize_mx(out=c_tile[:].bitcast(X4), scales=s_tile[:], in_=wgrp[e, g][:])
+            wcode[e, g] = keep.tile([P, R], U32, align_bytes=64, name="wcode%d%d" % (e, g))
+            wscale[e, g] = keep.tile([P, R], U8, align_bytes=64, name="wscale%d%d" % (e, g))
+            nc.vector.quantize_mx(out=wcode[e, g][:].bitcast(X4), scales=wscale[e, g][:], in_=wgrp[e, g][:])
 
-        pgrp = keep.tile([P, 2, 4 * E * F], BF16, align_bytes=64, name="pgrp")
-        pcode = keep.tile([P, 2, E * F], U32, align_bytes=64, name="pcode")
-        pscale = keep.tile([P, 2, E * F], U8, align_bytes=64, name="pscale")
+        gain = keep.tile([P, E * R], BF16, name="gain")
+
+        def order_gain():
+            nc.vector.tensor_copy(
+                out=gain[:].bitcast(F32).rearrange("q (e u p) -> q e u p", e=E, u=2),
+                in_=graw[:].bitcast(F32).rearrange("q (e p u) -> q e u p", e=E, u=2),
+            )
+
+        pgrp = keep.tile([P, 2 * 4 * E * F], BF16, align_bytes=64, name="pgrp")
+        pcode = keep.tile([P, 2 * E * F], U32, align_bytes=64, name="pcode")
+        pscale = keep.tile([P, 2 * E * F], U8, align_bytes=64, name="pscale")
         ugrp = keep.tile([P, 4 * E * F], BF16, align_bytes=64, name="ugrp")
         ucode = keep.tile([P, E * F], U32, align_bytes=64, name="ucode")
         uscale = keep.tile([P, E * F], U8, align_bytes=64, name="uscale")
 
         def group_p(g):
             nc.scalar.copy(
-                out=pgrp[:, g, :].rearrange("q (e f j) -> q e f j", e=E, j=4),
-                in_=praw[:, :, g].rearrange("q e j f -> q e f j"),
+                out=pgrp[:, 1024 * g : 1024 * (g + 1)].rearrange("q (e c i j) -> q e c j i", e=E, i=4, j=4),
+                in_=praw[:, :, g].rearrange("q e j (c i) -> q e c j i", i=4),
             )
-
-        def quant_p(g):
-            nc.vector.quantize_mx(out=pcode[:, g, :].bitcast(X4), scales=pscale[:, g, :], in_=pgrp[:, g, :])
 
         def group_u():
             nc.scalar.copy(
-                out=ugrp[:].rearrange("q (e f j) -> q e f j", e=E, j=4),
-                in_=uraw[:].rearrange("q e j f -> q e f j"),
+                out=ugrp[:].rearrange("q (e c i j) -> q e c j i", e=E, i=4, j=4),
+                in_=uraw[:].rearrange("q e j (c i) -> q e c j i", i=4),
             )
+
+        def quant_p():
+            nc.vector.quantize_mx(out=pcode[:].bitcast(X4), scales=pscale[:], in_=pgrp[:])
 
         def quant_u():
             nc.vector.quantize_mx(out=ucode[:].bitcast(X4), scales=uscale[:], in_=ugrp[:])
 
-        sums = []
-        clock = [0]
-        late = []
-
         xs, xt, xg, xc, xsc = {}, {}, {}, {}, {}
         acc, bb, bt, bg, bc, bsc = {}, {}, {}, {}, {}, {}
-        ACCS = 8 - 2 - TURN[1] - (TURN[3] if TURN[0] != TURN[2] else 0)
-        pps, ups, sil, q, z = {}, {}, {}, {}, {}
+        pps, ups, sil, q, z, res = {}, {}, {}, {}, {}, {}
         sumsq = keep.tile([P, TILES * E], F32, name="sumsq")
         gate = keep.tile([P, TILES, E], F32, name="gate")
 
         def scale_x(n):
-            k, m = n // 2, n % 2
-            if m == 0:
-                xs_tile = stage.tile([P, 2, D], BF16, align_bytes=64, name="xs", bufs=AHEAD // 2 + 2)
-                xs[k] = xs_tile
-            if n == 0:
-                for c in range(2):
-                    cols = slice(512 * c, 512 * (c + 1))
-                    nc.vector.tensor_tensor(out=xs[k][:, 0, cols], in0=xb[k][:, 0, cols].bitcast(F8), in1=xscale[:, 0, cols], op=ALU.mult)
-                return 1
-            if k < SINGLES:
-                nc.vector.tensor_tensor(out=xs[k][:, m, :], in0=xb[k][:, m, :].bitcast(F8), in1=xscale[:, 0, :], op=ALU.mult)
-                return 1
-            nc.vector.tensor_tensor(
-                out=xs[k][:].rearrange("q m d -> q (m d)"),
-                in0=xb[k][:].rearrange("q m d -> q (m d)").bitcast(F8),
-                in1=xscale[:].rearrange("q m d -> q (m d)"),
-                op=ALU.mult,
-            )
-            return 2
+            xs[n] = stage.tile([P, D], BF16, align_bytes=64, name="xs", bufs=HEAD_TILES + DOUBLE_STEPS - 4)
+            for cols in (slice(0, 512), slice(512, D)) if n == 0 else (slice(0, D),):
+                nc.vector.tensor_tensor(out=xs[n][:, cols], in0=xb[n // 2][:, n % 2, cols].bitcast(F8), in1=xscale[:, cols], op=ALU.mult)
 
-        def turn_x(n):
-            xt_tile = psum.tile([P, 2, 2, P], F32, name=TURN[0], bufs=TURN[1])
-            xt[n] = xt_tile
-            words = xs[n // 2][:, n % 2, :].bitcast(F32)
+        def turn_x(n, tag="xt"):
+            xt[n] = psum.tile([P, 2, 2, P], F32, name=tag)
+            words = xs[n][:].bitcast(F32)
             for g in range(2):
                 for u in range(2):
-                    nc.tensor.transpose(xt_tile[:, g, u, :], words[:, 256 * g + u : 256 * (g + 1) : 2], ident[:])
+                    nc.tensor.transpose(xt[n][:, g, u, :], words[:, 256 * g + u : 256 * (g + 1) : 2], ident[:])
 
         def leave_x(n):
             k, m = n // 2, n % 2
             if m == 0:
-                xg_tile = stage.tile([P, 2 * D], BF16, align_bytes=64, name="xg", bufs=3)
-                xg[k] = xg_tile
+                xg[k] = stage.tile([P, 2 * D], BF16, align_bytes=64, name="xg", bufs=2)
             nc.scalar.copy(
                 out=xg[k][:, D * m : D * (m + 1)].bitcast(F32).rearrange("q (g r u) -> q g r u", g=2, u=2),
                 in_=xt[n][:].rearrange("q g u r -> q g r u"),
             )
 
         def quant_x(k):
-            c_tile = keep.tile([P, 4 * P], U32, align_bytes=64, name="xc%d" % k)
-            s_tile = keep.tile([P, 4 * P], U8, align_bytes=64, name="xsc%d" % k)
-            xc[k], xsc[k] = c_tile, s_tile
-            nc.vector.quantize_mx(out=c_tile[:].bitcast(X4), scales=s_tile[:], in_=xg[k][:])
+            xc[k] = stage.tile([P, 4 * P], U32, align_bytes=64, name="xc", bufs=6)
+            xsc[k] = stage.tile([P, 4 * P], U8, align_bytes=64, name="xsc", bufs=6)
+            nc.vector.quantize_mx(out=xc[k][:].bitcast(X4), scales=xsc[k][:], in_=xg[k][:])
 
         def mm_a(n, e):
             k, m = n // 2, n % 2
-            a_tile = psum.tile([P, R], F32, name="acc", bufs=ACCS)
-            acc[n, e] = a_tile
+            acc[n, e] = psum.tile([P, R], F32, name="acc", bufs=4)
             for g in range(2):
                 cols = slice((2 * m + g) * P, (2 * m + g + 1) * P)
                 nc.tensor.matmul_mx(
-                    out=a_tile[:],
+                    out=acc[n, e][:],
                     lhsT=xc[k][:, cols].bitcast(X4),
                     lhsT_scale=xsc[k][:, cols],
                     rhs=wcode[e, g][:].bitcast(X4),
@@ -214,240 +170,297 @@ def tile_autonomyofexpertsnormgate_t_kernel(tc, x_bytes, x_scale, wdown, rgain, 
                     stop=(g == 1),
                 )
 
-        def gain_b(n, e):
-            if n not in bb:
-                bb_tile = stage.tile([P, E * R], BF16, align_bytes=64, name="bb", bufs=3)
-                bb[n] = bb_tile
-            nc.vector.tensor_tensor(
-                out=bb[n][:, e * R : (e + 1) * R].rearrange("q (u p i) -> q u p i", u=2, i=2),
-                in0=acc[n, e][:].rearrange("q (u i p) -> q u p i", u=2, i=2),
-                in1=gain[:, e].rearrange("q (p u) i -> q u p i", u=2),
-                op=ALU.mult,
-            )
-
-        def new_bg(k):
-            if k not in bg:
-                bg_tile = stage.tile([P, 2 * E * R], BF16, align_bytes=64, name="bg", bufs=3)
-                bg[k] = bg_tile
-
         def square(n, e):
             junk = stage.tile([P, R], BF16, name="junk", bufs=2)
             nc.scalar.activation(out=junk[:], in_=acc[n, e][:], func=ACT.Square, accum_out=sumsq[:, 2 * n + e : 2 * n + e + 1])
 
-        def turn_b(n):
-            bt_tile = psum.tile([P, E, 2, P], F32, name=TURN[2], bufs=TURN[3])
-            bt[n] = bt_tile
-            words = bb[n][:].bitcast(F32)
-            for e in range(E):
-                for u in range(2):
-                    nc.tensor.transpose(bt_tile[:, e, u, :], words[:, 256 * e + 128 * u : 256 * e + 128 * (u + 1)], ident[:])
+        def gain_b(n, e):
+            if e == 0:
+                bb[n] = stage.tile([P, E * R], BF16, align_bytes=64, name="bb", bufs=3)
+            cols = slice(e * R, (e + 1) * R)
+            nc.vector.tensor_tensor(out=bb[n][:, cols], in0=acc[n, e][:], in1=gain[:, cols], op=ALU.mult)
 
-        def leave_b(n):
-            k, m = n // 2, n % 2
-            ne = E
-            new_bg(k)
+        def turn_b(n, es=(0, 1), tag="bt"):
+            bt[n, es] = psum.tile([P, E, 2, P], F32, name=tag)
+            words = bb[n][:].bitcast(F32)
+            for e in es:
+                for u in range(2):
+                    nc.tensor.transpose(bt[n, es][:, e, u, :], words[:, 256 * e + 128 * u : 256 * e + 128 * (u + 1)], ident[:])
+
+        def leave_b(n, es=(0, 1)):
+            k, first = n // 2, 2 * (n % 2) + es[0]
+            if first == 0:
+                bg[k] = stage.tile([P, 2 * E * R], BF16, align_bytes=64, name="bg", bufs=2)
             nc.scalar.copy(
-                out=bg[k][:, E * R * m : E * R * m + ne * R].bitcast(F32).rearrange("q (e r u) -> q e r u", e=ne, u=2),
-                in_=bt[n][:, 0:ne].rearrange("q e u r -> q e r u"),
+                out=bg[k][:, R * first : R * (first + len(es))].bitcast(F32).rearrange("q (e r u) -> q e r u", e=len(es), u=2),
+                in_=bt[n, es][:, es[0] : es[0] + len(es)].rearrange("q e u r -> q e r u"),
             )
 
-        def quant_b(k):
-            c_tile = keep.tile([P, 4 * P], U32, align_bytes=64, name="bc%d" % k)
-            s_tile = keep.tile([P, 4 * P], U8, align_bytes=64, name="bsc%d" % k)
-            bc[k], bsc[k] = c_tile, s_tile
-            nc.vector.quantize_mx(out=c_tile[:].bitcast(X4), scales=s_tile[:], in_=bg[k][:])
+        def quant_b(k, first=0, count=4):
+            if first == 0:
+                bc[k] = stage.tile([P, 4 * P], U32, align_bytes=64, name="bc", bufs=2)
+                bsc[k] = stage.tile([P, 4 * P], U8, align_bytes=64, name="bsc", bufs=2)
+            cols = slice(P * first, P * (first + count))
+            nc.vector.quantize_mx(out=bc[k][:, cols].bitcast(X4), scales=bsc[k][:, cols], in_=bg[k][:, R * first : R * (first + count)])
 
-        def mm_final(k):
-            p_tile = psum.tile([P, 2, E * F], F32, name="pp")
-            u_tile = psum.tile([P, 2, E, F], F32, name="uu")
-            pps[k], ups[k] = p_tile, u_tile
-            for m in range(2):
-                for e in range(E):
-                    cols = slice((2 * m + e) * P, (2 * m + e + 1) * P)
-                    ecols = slice(e * F, (e + 1) * F)
-                    nc.tensor.matmul_mx(
-                        out=u_tile[:, m, e, :],
-                        lhsT=bc[k][:, cols].bitcast(X4),
-                        lhsT_scale=bsc[k][:, cols],
-                        rhs=ucode[:, ecols].bitcast(X4),
-                        rhs_scale=uscale[:, ecols],
-                        start=True,
-                        stop=True,
-                    )
+        def bank(tag):
+            tile = psum.tile([P, 4 * F], F32, name=tag, bufs=4 if tag == "acc" else 1)
+            return tile
+
+        def mm_u(k, first=0, count=4, tag="uu"):
+            ups[k, first] = bank(tag)
+            for slot in range(first, first + count):
+                cols = slice(slot * P, (slot + 1) * P)
+                ecols = slice(slot % E * F, (slot % E + 1) * F)
+                nc.tensor.matmul_mx(
+                    out=ups[k, first][:, cols],
+                    lhsT=bc[k][:, cols].bitcast(X4),
+                    lhsT_scale=bsc[k][:, cols],
+                    rhs=ucode[:, ecols].bitcast(X4),
+                    rhs_scale=uscale[:, ecols],
+                    start=True,
+                    stop=True,
+                )
+
+        def mm_p(k, tag="pp"):
+            pps[k] = bank(tag)
             for m in range(2):
                 for g in range(2):
                     cols = slice((2 * m + g) * P, (2 * m + g + 1) * P)
+                    gcols = slice(g * E * F, (g + 1) * E * F)
                     nc.tensor.matmul_mx(
-                        out=p_tile[:, m, :],
+                        out=pps[k][:, m * E * F : (m + 1) * E * F],
                         lhsT=xc[k][:, cols].bitcast(X4),
                         lhsT_scale=xsc[k][:, cols],
-                        rhs=pcode[:, g, :].bitcast(X4),
-                        rhs_scale=pscale[:, g, :],
+                        rhs=pcode[:, gcols].bitcast(X4),
+                        rhs_scale=pscale[:, gcols],
                         start=(g == 0),
                         stop=(g == 1),
                     )
 
-        def silu(k):
-            s_tile = stage.tile([P, 2, E, F], F32, name="sil", bufs=2)
-            sil[k] = s_tile
-            nc.scalar.activation(out=s_tile[:], in_=ups[k][:], func=ACT.Silu)
+        def silu(k, first=0, count=4):
+            cols = slice(F * first, F * (first + count))
+            if first == 0:
+                sil[k] = stage.tile([P, 4 * F], F32, name="sil", bufs=2)
+            nc.scalar.activation(out=sil[k][:, cols], in_=ups[k, first][:, cols], func=ACT.Silu)
 
-        def mix(k):
-            q_tile = stage.tile([P, 2, E, F], F32, name="q", bufs=3)
-            q[k] = q_tile
-            nc.vector.tensor_tensor(
-                out=q_tile[:].rearrange("q m e f -> q (m e f)"),
-                in0=sil[k][:].rearrange("q m e f -> q (m e f)"),
-                in1=pps[k][:].rearrange("q m f -> q (m f)"),
-                op=ALU.mult,
+        def mix(k, first=0, count=4):
+            cols = slice(F * first, F * (first + count))
+            if first == 0:
+                q[k] = stage.tile([P, 4 * F], F32, name="q", bufs=13)
+            nc.vector.tensor_tensor(out=q[k][:, cols], in0=sil[k][:, cols], in1=pps[k][:, cols], op=ALU.mult)
+
+        def weigh(n):
+            k, m = n // 2, n % 2
+            z[n] = stage.tile([P, F], F32, name="z", bufs=24)
+            nc.scalar.activation(out=z[n][:], in_=q[k][:, (2 * m + 1) * F : (2 * m + 2) * F], func=ACT.Copy, scale=gate[:, n, 1:2])
+
+        def store(k, ms):
+            rows = out[256 * k : 256 * k + 256, :].rearrange("(p m) f -> p m f", m=2)
+            nc.sync.dma_start(out=rows[:, ms], in_=res[k][:, ms])
+
+        def join(n):
+            k, m = n // 2, n % 2
+            if m == 0:
+                res[k] = stage.tile([P, 2, F], F32, name="res", bufs=6)
+            nc.vector.scalar_tensor_tensor(
+                out=res[k][:, m, :],
+                in0=q[k][:, 2 * m * F : (2 * m + 1) * F],
+                scalar=gate[:, n, 0:1],
+                in1=z[n][:],
+                op0=ALU.mult,
+                op1=ALU.add,
             )
-
-        def weigh(k):
-            z_tile = stage.tile([P, 2, F], F32, name="z", bufs=3)
-            z[k] = z_tile
-            for m in range(2):
-                nc.scalar.activation(out=z_tile[:, m, :], in_=q[k][:, m, 1, :], func=ACT.Copy, scale=gate[:, 2 * k + m, 1:2])
-
-        def join(k):
-            o = stage.tile([P, 2, F], F32, name="o", bufs=3)
-            for m in range(2):
-                nc.vector.scalar_tensor_tensor(
-                    out=o[:, m, :], in0=q[k][:, m, 0, :], scalar=gate[:, 2 * k + m, 0:1], in1=z[k][:, m, :], op0=ALU.mult, op1=ALU.add
-                )
-            nc.sync.dma_start(out=out[256 * k : 256 * k + 256, :].rearrange("(p m) f -> p m f", m=2), in_=o[:])
+            if m == 1:
+                store(k, slice(0, 2))
 
         def gate_steps(first, count):
             t0, nt = 2 * first, 2 * count
             ss = sumsq[:, E * t0 : E * (t0 + nt)]
             seed = stage.tile([P, E * nt], I32, name="seed", bufs=2)
+            diff = stage.tile([P, nt], F32, name="diff", bufs=2)
             state = {"y": seed[:].bitcast(F32)}
 
             def start():
                 nc.vector.tensor_scalar(out=seed[:], in0=ss.bitcast(I32), scalar1=0.5, scalar2=SQRT_SEED, op0=ALU.mult, op1=ALU.add)
 
             def recip():
-                r = stage.tile([P, E * nt], F32, name="newton_r", bufs=2)
-                state["r"] = r
-                nc.vector.reciprocal(out=r[:], in_=state["y"])
+                state["r"] = stage.tile([P, E * nt], F32, name="heron_r", bufs=2)
+                nc.vector.reciprocal(out=state["r"][:], in_=state["y"])
 
             def divide():
-                t = stage.tile([P, E * nt], F32, name="newton_t", bufs=2)
-                state["t"] = t
-                nc.vector.scalar_tensor_tensor(out=t[:], in0=ss, scalar=0.5, in1=state["r"][:], op0=ALU.mult, op1=ALU.mult)
+                state["t"] = stage.tile([P, E * nt], F32, name="heron_t", bufs=2)
+                nc.vector.scalar_tensor_tensor(out=state["t"][:], in0=ss, scalar=0.5, in1=state["r"][:], op0=ALU.mult, op1=ALU.mult)
 
             def average():
-                y = stage.tile([P, E * nt], F32, name="newton_y", bufs=2)
+                y = stage.tile([P, E * nt], F32, name="heron_y", bufs=2)
                 nc.vector.scalar_tensor_tensor(out=y[:], in0=state["y"], scalar=0.5, in1=state["t"][:], op0=ALU.mult, op1=ALU.add)
                 state["y"] = y[:]
 
-            def finish():
-                d = stage.tile([P, nt], F32, name="gate_d", bufs=2)
-                h = stage.tile([P, nt], F32, name="gate_h", bufs=2)
+            def subtract():
                 both = state["y"].rearrange("q (n e) -> q e n", e=E)
-                nc.vector.tensor_tensor(out=d[:], in0=both[:, 0], in1=both[:, 1], op=ALU.subtract)
-                late.append((clock[0] + LATE, lambda: squash(d, h)))
+                nc.vector.tensor_tensor(out=diff[:], in0=both[:, 0], in1=both[:, 1], op=ALU.subtract)
+                squashes.append(squash)
 
-            def squash(d, h):
-                nc.scalar.activation(out=h[:], in_=d[:], func=ACT.Tanh, scale=0.5)
+            def squash():
+                h = stage.tile([P, nt], F32, name="tanh", bufs=2)
+                nc.scalar.activation(out=h[:], in_=diff[:], func=ACT.Tanh, scale=0.5)
                 for e in range(E):
                     nc.scalar.activation(out=gate[:, t0 : t0 + nt, e], in_=h[:], func=ACT.Copy, scale=(0.5, -0.5)[e], bias=0.5)
-                ready.extend(range(first, first + count))
+                gated.extend(range(t0, t0 + nt))
 
-            return [start] + [recip, divide, average] * 3 + [finish]
+            return [start] + [recip, divide, average] * 3 + [subtract]
 
-        silus = []
-        scales = []
-        small = []
-        ready = []
-        final = []
-        bounds, total = {}, 0
-        for count in GROUPS:
-            bounds[2 * (total + count) - 1] = (total, count)
-            total += count
+        scaled = []
 
-        def weave(count):
+        def scale_next(count):
             for i in range(count):
-                if small:
-                    small.pop(0)()
+                scale_x(len(scaled))
+                scaled.append(True)
 
-        done = 0
-        s = -AHEAD
-        waiting = []
-        scaled = 0
-        while done < PAIRS:
-            clock[0] = s
-            busy = 0 <= s < TILES
-            for tok in (TAIL if s >= TILES else LATEST if s >= LS else STEP):
-                if tok == "TX" and 0 <= s + LTX < TILES:
-                    turn_x(s + LTX)
-                elif tok == "LX" and 0 <= s + LLX < TILES:
-                    leave_x(s + LLX)
-                elif tok == "TB" and 0 <= s - LTB < TILES:
-                    turn_b(s - LTB)
-                elif tok == "LB" and 0 <= s - LLB < TILES:
-                    leave_b(s - LLB)
-                elif tok == "G0" and busy:
-                    gain_b(s, 0)
-                elif tok == "G1" and busy:
-                    gain_b(s, 1)
-                elif tok == "S0" and busy:
-                    square(s, 0)
-                elif tok == "S1" and busy:
-                    square(s, 1)
-                elif tok == "M0" and 0 <= s + LMA < TILES:
-                    mm_a(s + LMA, 0)
-                elif tok == "M1" and 0 <= s + LMA < TILES:
-                    mm_a(s + LMA, 1)
-                elif tok == "SX" and scaled < TILES and (scaled - AHEAD <= s if s < 0 else (scaled - AHEAD) * PACE <= s):
-                    scaled += scale_x(scaled)
-                elif tok == "N":
-                    weave(1)
-                elif tok == "MX" and final:
-                    mix(final[0])
-                    scales.append(final[0])
-                    sums.append(final.pop(0))
-                    done += 1
-                elif tok == "ZS" and scales:
-                    weigh(scales.pop(0))
-                elif tok == "AD" and sums and sums[0] not in scales:
-                    join(sums.pop(0))
-                elif tok == "LA" and late and (s >= late[0][0] or s >= TILES):
-                    late.pop(0)[1]()
-                elif tok == "QX" and (s + LQX) % 2 == 0 and 0 <= (s + LQX) // 2 < PAIRS:
-                    quant_x((s + LQX) // 2)
-                elif tok == "QB" and (s - LQB) % 2 == 0 and 0 <= (s - LQB) // 2 < PAIRS:
-                    quant_b((s - LQB) // 2)
-                elif tok == "W":
-                    for w in range(WPER * (s + AHEAD - WFROM), WPER * (s + AHEAD - WFROM + 1)):
-                        if 0 <= w < 8:
-                            group_w(WENG[w], w // 4, w // 2 % 2, w % 2)
-                elif tok == "WQ":
-                    for w in range(WPER * (s + AHEAD - WFROM - WLAG), WPER * (s + AHEAD - WFROM - WLAG + 1)):
-                        if 0 <= w < 8 and w % 2 == 1:
-                            quant_w(w // 4, w // 2 % 2)
-                    if s in (1, 2):
-                        group_p(s - 1)
-                    if s == 3:
-                        group_u()
-                elif tok == "QW":
-                    if s in (4, 5):
-                        quant_p(s - 4)
-                    if s == 6:
-                        quant_u()
-                elif tok == "MF":
-                    if ready and ready[0] in bc and not final and (s >= 2 * ready[0] + FLAG or s >= TILES - FEND):
-                        k = ready.pop(0)
-                        mm_final(k)
-                        final.append(k)
-                        silus.append(k)
-                elif tok == "SI" and silus:
-                    silu(silus.pop(0))
-            if s in bounds:
-                waiting.append((s + SEED, bounds[s]))
-            if waiting and waiting[0][0] <= s:
-                small.extend(gate_steps(*waiting.pop(0)[1]))
-            s += 1
-        while scales:
-            weigh(scales.pop(0))
-        while sums:
-            join(sums.pop(0))
+        blocks = [(e, g) for e in range(E) for g in range(2)]
+        scale_next(4)
+        for i in range(4):
+            group_w(*blocks[i])
+            if i < 3:
+                turn_x(2 * i)
+                turn_x(2 * i + 1, "bt")
+                leave_x(2 * i)
+                leave_x(2 * i + 1)
+            else:
+                group_u()
+                order_gain()
+            quant_w(*blocks[i])
+            if i % 2 == 1:
+                for n in range(2):
+                    mm_a(n, i // 2)
+            scale_next(1)
+            if i < 3:
+                quant_x(i)
+            else:
+                quant_u()
+            scale_next(1)
+        for e in range(E):
+            square(0, e)
+
+        small, fresh, squashes, gated, mixed, weighed = [], [], [], [], [], []
+        ends, total = {}, 0
+        for count in GROUPS:
+            ends[2 * (total + count) - 1] = (total, count)
+            total += count
+        last = PAIRS - 1
+
+        def weave():
+            if small:
+                small.pop(0)()
+
+        def weigh_ready(count):
+            for i in range(count):
+                if gated and gated[0] in mixed:
+                    weighed.append(gated[0])
+                    weigh(gated.pop(0))
+
+        for s in range(TILES - 1):
+            joins = weighed[:JOINS] if len(scaled) == TILES else []
+            weighed[:] = weighed[len(joins) :]
+            gain_b(s, 0)
+            weave()
+            gain_b(s, 1)
+            weave()
+            if s + 1 < TILES:
+                for e in range(E):
+                    square(s + 1, e)
+            if s + 1 in ends:
+                fresh.extend(gate_steps(*ends[s + 1]))
+            if s % 2 == 0 and s >= 4:
+                silu((s - 4) // 2)
+            if s + TURN_AHEAD < TILES:
+                turn_x(s + TURN_AHEAD)
+            if s >= 1:
+                turn_b(s - 1)
+            if s + TURN_AHEAD < TILES:
+                leave_x(s + TURN_AHEAD)
+            if s >= 1:
+                leave_b(s - 1)
+            if squashes:
+                squashes.pop(0)()
+            else:
+                weigh_ready(2)
+            if s in (0, 1):
+                group_p(s)
+            if s == 2:
+                quant_p()
+            if s % 2 == 1 and s >= 3:
+                quant_b((s - 3) // 2)
+            if s % 2 == 0 and 3 <= (s + 4) // 2 < PAIRS:
+                quant_x((s + 4) // 2)
+            weave()
+            if s + 2 < TILES:
+                for e in range(E):
+                    mm_a(s + 2, e)
+            if s % 2 == 1 and s >= 3:
+                mm_u((s - 3) // 2)
+                mm_p((s - 3) // 2)
+            lead = HEAD_TILES + 2 * DOUBLE_STEPS
+            for i in range(2 if s < DOUBLE_STEPS else 1):
+                if len(scaled) < TILES and (len(scaled) - lead) * (TILES - TURN_AHEAD - 1 - DOUBLE_STEPS) <= (s - DOUBLE_STEPS) * (TILES - lead):
+                    scale_next(1)
+                    weave()
+            for n in joins:
+                join(n)
+            small.extend(fresh)
+            fresh.clear()
+            if joins:
+                weave()
+            if s % 2 == 0 and s >= 4:
+                mix((s - 4) // 2)
+                mixed.extend((s - 4, s - 3))
+                weave()
+
+        n = TILES - 1
+        turn_b(n - 1, tag="xt")
+        leave_b(n - 1)
+        quant_b(last - 1)
+        weave()
+        mm_u(last - 1)
+        mm_p(last - 1)
+        gain_b(n, 0)
+        weave()
+        silu(last - 1)
+        quant_b(last, 0, 2)
+        weave()
+        gain_b(n, 1)
+        weave()
+        turn_b(n, (0,))
+        mm_u(last, 0, 2, "acc")
+        mm_p(last, "acc")
+        turn_b(n, (1,), "xt")
+        leave_b(n, (0,))
+        silu(last, 0, 2)
+        leave_b(n, (1,))
+        mix(last - 1)
+        weave()
+        quant_b(last, 2, 1)
+        weave()
+        mix(last, 0, 2)
+        weave()
+        quant_b(last, 3, 1)
+        mixed.extend(range(n - 3, n))
+        mm_u(last, 2, 1)
+        mm_u(last, 3, 1, "acc")
+        while small:
+            weave()
+        silu(last, 2, 1)
+        squashes.pop()()
+        silu(last, 3, 1)
+        weigh_ready(TILES)
+        for m in weighed:
+            join(m)
+        store(last, slice(0, 1))
+        for e in range(E):
+            cols = slice((2 + e) * F, (3 + e) * F)
+            nc.vector.scalar_tensor_tensor(
+                out=q[last][:, cols], in0=pps[last][:, cols], scalar=gate[:, n, e : e + 1], in1=sil[last][:, cols], op0=ALU.mult, op1=ALU.mult
+            )
+        nc.vector.tensor_tensor(out=res[last][:, 1, :], in0=q[last][:, 2 * F : 3 * F], in1=q[last][:, 3 * F : 4 * F], op=ALU.add)
+        store(last, slice(1, 2))

@@ -22,10 +22,7 @@ ALU = mybir.AluOpType
 SQRT_SEED = 532487669.0
 GROUPS = (6, 6, 4)
 TURN_AHEAD = 6
-HEAD_TILES = 12
-DOUBLE_STEPS = 2
-WEIGHT_ENGINES = "ssss"
-JOINS = 4
+JOINS = 3
 
 
 def tile_autonomyofexpertsnormgate_t_kernel(tc, x_bytes, x_scale, wdown, rgain, wup, wp, out):
@@ -36,7 +33,7 @@ def tile_autonomyofexpertsnormgate_t_kernel(tc, x_bytes, x_scale, wdown, rgain, 
         psum = ctx.enter_context(tc.psum_pool(name="psum", bufs=1))
         ctx.enter_context(tc.manual_schedule())
 
-        xscale = keep.tile([P, D], F32, name="xscale")
+        xscale = keep.tile([P, 2 * D], F32, name="xscale")
         xb, wraw = {}, {}
 
         def load_x(k):
@@ -47,20 +44,19 @@ def tile_autonomyofexpertsnormgate_t_kernel(tc, x_bytes, x_scale, wdown, rgain, 
             wraw[e, g] = keep.tile([P, 4, R], BF16, name="wraw%d%d" % (e, g))
             nc.sync.dma_start(out=wraw[e, g][:], in_=wdown[e, 512 * g : 512 * g + 512, :].rearrange("(p j) c -> p j c", j=4))
 
-        spread = x_scale.rearrange("o k -> (o k)")
+        sraw = keep.tile([P, 2, 8], F32, name="sraw")
+        nc.sync.dma_start(out=sraw[:, :, 0:4], in_=x_scale.rearrange("o (g p t) -> p (o g) t", g=2, t=4))
+        graw = keep.tile([P, E, 16], BF16, name="graw")
+        nc.sync.dma_start(out=graw[:, :, 0:4], in_=rgain.rearrange("e (p t) -> p e t", t=4))
         xb[0] = keep.tile([P, 2, D], U8, name="xb0")
-        for half in range(2):
-            cols = slice(512 * half, 512 * half + 512)
-            nc.sync.dma_start(out=xscale[:, cols], in_=spread[cols].partition_broadcast(P))
-            nc.sync.dma_start(out=xb[0][:, half, :], in_=x_bytes[0:256, :].rearrange("(p m) d -> p m d", m=2)[:, half, :])
+        for m in range(2):
+            nc.sync.dma_start(out=xb[0][:, m, :], in_=x_bytes[0:256, :].rearrange("(p m) d -> p m d", m=2)[:, m, :])
         load_w(0, 0)
         load_x(1)
         load_w(0, 1)
         load_w(1, 0)
         load_x(2)
         load_w(1, 1)
-        graw = keep.tile([P, E * R], BF16, name="graw")
-        nc.sync.dma_start(out=graw[:], in_=rgain.rearrange("e r -> (e r)").partition_broadcast(P))
         load_x(3)
         load_x(4)
         praw = keep.tile([P, E, 2, 4, F], BF16, name="praw")
@@ -73,17 +69,35 @@ def tile_autonomyofexpertsnormgate_t_kernel(tc, x_bytes, x_scale, wdown, rgain, 
 
         ident = keep.tile([P, P], F32, name="ident")
         make_identity(nc, ident[:])
+        ident16 = keep.tile([P, P], BF16, name="ident16")
+        make_identity(nc, ident16[:])
+
+        def spread(column, place):
+            nc.tensor.transpose(place, column.to_broadcast([P, P]), ident[:])
+
+        turned = {}
+        for g in range(2):
+            turned[g] = psum.tile([P, 4, P], F32, name=("xt", "bt")[g])
+            for t in range(4):
+                spread(sraw[:, g, t : t + 1], turned[g][:, t, :])
+        for m in range(2):
+            for g in range(2):
+                dst = xscale[:, D * m + 512 * g : D * m + 512 * (g + 1)].rearrange("q (p t) -> q p t", t=4)
+                nc.scalar.copy(out=dst, in_=turned[g][:].rearrange("q t p -> q p t"))
 
         wgrp, wcode, wscale = {}, {}, {}
 
+        def interleave(dst, sources, tag):
+            laid = psum.tile([P, 1024], BF16, name=tag)
+            for h in range(2):
+                nc.tensor.matmul(laid[:, 512 * h : 512 * (h + 1)], lhsT=ident16[:], rhs=sources[h], start=True, stop=True)
+            nc.scalar.copy(out=dst, in_=laid[:])
+
         def group_w(e, g):
             wgrp[e, g] = stage.tile([P, 4 * R], BF16, align_bytes=64, name="wgrp", bufs=2)
-            dst = wgrp[e, g][:].rearrange("q (u p i j) -> q p j u i", u=2, i=2, j=4)
-            src = wraw[e, g][:].rearrange("q j (p u i) -> q p j u i", u=2, i=2)
-            if WEIGHT_ENGINES[2 * e + g] == "s":
-                nc.scalar.copy(out=dst, in_=src)
-            else:
-                nc.vector.tensor_copy(out=dst, in_=src)
+            src = wraw[e, g][:].rearrange("q j (p u i) -> q u p i j", u=2, i=2)
+            for u in range(2):
+                interleave(wgrp[e, g][:, 1024 * u : 1024 * (u + 1)], [src[:, u, 0:64], src[:, u, 64:128]], ("uu", "pp")[u])
 
         def quant_w(e, g):
             wcode[e, g] = keep.tile([P, R], U32, align_bytes=64, name="wcode%d%d" % (e, g))
@@ -92,11 +106,13 @@ def tile_autonomyofexpertsnormgate_t_kernel(tc, x_bytes, x_scale, wdown, rgain, 
 
         gain = keep.tile([P, E * R], BF16, name="gain")
 
-        def order_gain():
-            nc.vector.tensor_copy(
-                out=gain[:].bitcast(F32).rearrange("q (e u p) -> q e u p", e=E, u=2),
-                in_=graw[:].bitcast(F32).rearrange("q (e p u) -> q e u p", e=E, u=2),
-            )
+        def spread_gain():
+            spread_words = psum.tile([P, E, 2, P], F32, name="xt")
+            words = graw[:].bitcast(F32)
+            for e in range(E):
+                for u in range(2):
+                    spread(words[:, e, u : u + 1], spread_words[:, e, u, :])
+            nc.scalar.copy(out=gain[:].bitcast(F32), in_=spread_words[:].rearrange("q e u p -> q (e u p)"))
 
         pgrp = keep.tile([P, 2 * 4 * E * F], BF16, align_bytes=64, name="pgrp")
         pcode = keep.tile([P, 2 * E * F], U32, align_bytes=64, name="pcode")
@@ -106,16 +122,10 @@ def tile_autonomyofexpertsnormgate_t_kernel(tc, x_bytes, x_scale, wdown, rgain, 
         uscale = keep.tile([P, E * F], U8, align_bytes=64, name="uscale")
 
         def group_p(g):
-            nc.scalar.copy(
-                out=pgrp[:, 1024 * g : 1024 * (g + 1)].rearrange("q (e c i j) -> q e c j i", e=E, i=4, j=4),
-                in_=praw[:, :, g].rearrange("q e j (c i) -> q e c j i", i=4),
-            )
+            interleave(pgrp[:, 1024 * g : 1024 * (g + 1)], [praw[:, e, g].rearrange("q j f -> q f j") for e in range(E)], ("uu", "pp")[g])
 
         def group_u():
-            nc.scalar.copy(
-                out=ugrp[:].rearrange("q (e c i j) -> q e c j i", e=E, i=4, j=4),
-                in_=uraw[:].rearrange("q e j (c i) -> q e c j i", i=4),
-            )
+            interleave(ugrp[:], [uraw[:, e].rearrange("q j f -> q f j") for e in range(E)], "uu")
 
         def quant_p():
             nc.vector.quantize_mx(out=pcode[:].bitcast(X4), scales=pscale[:], in_=pgrp[:])
@@ -129,14 +139,18 @@ def tile_autonomyofexpertsnormgate_t_kernel(tc, x_bytes, x_scale, wdown, rgain, 
         sumsq = keep.tile([P, TILES * E], F32, name="sumsq")
         gate = keep.tile([P, TILES, E], F32, name="gate")
 
-        def scale_x(n):
-            xs[n] = stage.tile([P, D], BF16, align_bytes=64, name="xs", bufs=HEAD_TILES + DOUBLE_STEPS - 4)
-            for cols in (slice(0, 512), slice(512, D)) if n == 0 else (slice(0, D),):
-                nc.vector.tensor_tensor(out=xs[n][:, cols], in0=xb[n // 2][:, n % 2, cols].bitcast(F8), in1=xscale[:, cols], op=ALU.mult)
+        def scale_x(k):
+            xs[k] = stage.tile([P, 2 * D], BF16, align_bytes=64, name="xs", bufs=5)
+            if k == 0:
+                for m, cols in ((0, slice(0, 512)), (0, slice(512, D)), (1, slice(0, D))):
+                    dst = xs[k][:, D * m + cols.start : D * m + cols.stop]
+                    nc.vector.tensor_tensor(out=dst, in0=xb[k][:, m, cols].bitcast(F8), in1=xscale[:, cols], op=ALU.mult)
+                return
+            nc.vector.tensor_tensor(out=xs[k][:], in0=xb[k][:].rearrange("q m d -> q (m d)").bitcast(F8), in1=xscale[:], op=ALU.mult)
 
         def turn_x(n, tag="xt"):
             xt[n] = psum.tile([P, 2, 2, P], F32, name=tag)
-            words = xs[n][:].bitcast(F32)
+            words = xs[n // 2][:, D * (n % 2) : D * (n % 2 + 1)].bitcast(F32)
             for g in range(2):
                 for u in range(2):
                     nc.tensor.transpose(xt[n][:, g, u, :], words[:, 256 * g + u : 256 * (g + 1) : 2], ident[:])
@@ -155,9 +169,14 @@ def tile_autonomyofexpertsnormgate_t_kernel(tc, x_bytes, x_scale, wdown, rgain, 
             xsc[k] = stage.tile([P, 4 * P], U8, align_bytes=64, name="xsc", bufs=6)
             nc.vector.quantize_mx(out=xc[k][:].bitcast(X4), scales=xsc[k][:], in_=xg[k][:])
 
+        def bank(tag):
+            tile = psum.tile([P, 4 * F], F32, name=tag, bufs=4 if tag == "acc" else 1)
+            return tile
+
         def mm_a(n, e):
             k, m = n // 2, n % 2
-            acc[n, e] = psum.tile([P, R], F32, name="acc", bufs=4)
+            if (n, e) not in acc:
+                acc[n, e] = bank("acc")
             for g in range(2):
                 cols = slice((2 * m + g) * P, (2 * m + g + 1) * P)
                 nc.tensor.matmul_mx(
@@ -202,10 +221,6 @@ def tile_autonomyofexpertsnormgate_t_kernel(tc, x_bytes, x_scale, wdown, rgain, 
                 bsc[k] = stage.tile([P, 4 * P], U8, align_bytes=64, name="bsc", bufs=2)
             cols = slice(P * first, P * (first + count))
             nc.vector.quantize_mx(out=bc[k][:, cols].bitcast(X4), scales=bsc[k][:, cols], in_=bg[k][:, R * first : R * (first + count)])
-
-        def bank(tag):
-            tile = psum.tile([P, 4 * F], F32, name=tag, bufs=4 if tag == "acc" else 1)
-            return tile
 
         def mm_u(k, first=0, count=4, tag="uu"):
             ups[k, first] = bank(tag)
@@ -313,35 +328,44 @@ def tile_autonomyofexpertsnormgate_t_kernel(tc, x_bytes, x_scale, wdown, rgain, 
 
         scaled = []
 
-        def scale_next(count):
-            for i in range(count):
-                scale_x(len(scaled))
-                scaled.append(True)
+        def scale_next():
+            scale_x(len(scaled))
+            scaled.append(True)
 
-        blocks = [(e, g) for e in range(E) for g in range(2)]
-        scale_next(4)
-        for i in range(4):
-            group_w(*blocks[i])
-            if i < 3:
-                turn_x(2 * i)
-                turn_x(2 * i + 1, "bt")
-                leave_x(2 * i)
-                leave_x(2 * i + 1)
-            else:
-                group_u()
-                order_gain()
-            quant_w(*blocks[i])
-            if i % 2 == 1:
-                for n in range(2):
-                    mm_a(n, i // 2)
-            scale_next(1)
-            if i < 3:
-                quant_x(i)
-            else:
-                quant_u()
-            scale_next(1)
-        for e in range(E):
-            square(0, e)
+        def turn_pair(k):
+            turn_x(2 * k)
+            turn_x(2 * k + 1, "bt")
+            leave_x(2 * k)
+            leave_x(2 * k + 1)
+
+        scale_next()
+        scale_next()
+        group_w(0, 0)
+        turn_pair(0)
+        group_w(0, 1)
+        quant_w(0, 0)
+        quant_x(0)
+        group_w(1, 0)
+        quant_w(0, 1)
+        turn_pair(1)
+        spread_gain()
+        scale_next()
+        group_w(1, 1)
+        quant_w(1, 0)
+        quant_x(1)
+        for n in range(2):
+            for e in range(E):
+                acc[n, e] = bank("acc")
+        for n in range(2):
+            mm_a(n, 0)
+        square(0, 0)
+        turn_pair(2)
+        scale_next()
+        quant_w(1, 1)
+        for n in range(2):
+            mm_a(n, 1)
+        square(0, 1)
+        scale_next()
 
         small, fresh, squashes, gated, mixed, weighed = [], [], [], [], [], []
         ends, total = {}, 0
@@ -361,7 +385,7 @@ def tile_autonomyofexpertsnormgate_t_kernel(tc, x_bytes, x_scale, wdown, rgain, 
                     weigh(gated.pop(0))
 
         for s in range(TILES - 1):
-            joins = weighed[:JOINS] if len(scaled) == TILES else []
+            joins = weighed[:JOINS] if len(scaled) == PAIRS else []
             weighed[:] = weighed[len(joins) :]
             gain_b(s, 0)
             weave()
@@ -385,14 +409,22 @@ def tile_autonomyofexpertsnormgate_t_kernel(tc, x_bytes, x_scale, wdown, rgain, 
             if squashes:
                 squashes.pop(0)()
             else:
-                weigh_ready(2)
-            if s in (0, 1):
-                group_p(s)
+                weigh_ready(3)
+            if s == 0:
+                group_u()
+                group_p(1)
+            if s == 1:
+                group_p(0)
+                quant_u()
             if s == 2:
                 quant_p()
             if s % 2 == 1 and s >= 3:
                 quant_b((s - 3) // 2)
-            if s % 2 == 0 and 3 <= (s + 4) // 2 < PAIRS:
+            if s % 2 == 1 and s >= 5:
+                weave()
+                mix((s - 5) // 2)
+                mixed.extend((s - 5, s - 4))
+            if s % 2 == 0 and (s + 4) // 2 < PAIRS:
                 quant_x((s + 4) // 2)
             weave()
             if s + 2 < TILES:
@@ -401,66 +433,48 @@ def tile_autonomyofexpertsnormgate_t_kernel(tc, x_bytes, x_scale, wdown, rgain, 
             if s % 2 == 1 and s >= 3:
                 mm_u((s - 3) // 2)
                 mm_p((s - 3) // 2)
-            lead = HEAD_TILES + 2 * DOUBLE_STEPS
-            for i in range(2 if s < DOUBLE_STEPS else 1):
-                if len(scaled) < TILES and (len(scaled) - lead) * (TILES - TURN_AHEAD - 1 - DOUBLE_STEPS) <= (s - DOUBLE_STEPS) * (TILES - lead):
-                    scale_next(1)
-                    weave()
+            if s % 2 == 1 and len(scaled) < PAIRS:
+                scale_next()
+                weave()
             for n in joins:
                 join(n)
-            small.extend(fresh)
-            fresh.clear()
             if joins:
                 weave()
-            if s % 2 == 0 and s >= 4:
-                mix((s - 4) // 2)
-                mixed.extend((s - 4, s - 3))
-                weave()
+            small.extend(fresh)
+            fresh.clear()
 
         n = TILES - 1
+        gain_b(n, 0)
+        weave()
         turn_b(n - 1, tag="xt")
         leave_b(n - 1)
+        mm_p(last - 1, "acc")
+        mm_p(last, "acc")
+        gain_b(n, 1)
+        weave()
+        turn_b(n)
+        leave_b(n)
+        mix(last - 2)
+        weave()
         quant_b(last - 1)
         weave()
         mm_u(last - 1)
-        mm_p(last - 1)
-        gain_b(n, 0)
-        weave()
-        silu(last - 1)
         quant_b(last, 0, 2)
         weave()
-        gain_b(n, 1)
+        quant_b(last, 2, 2)
         weave()
-        turn_b(n, (0,))
-        mm_u(last, 0, 2, "acc")
-        mm_p(last, "acc")
-        turn_b(n, (1,), "xt")
-        leave_b(n, (0,))
-        silu(last, 0, 2)
-        leave_b(n, (1,))
-        mix(last - 1)
-        weave()
-        quant_b(last, 2, 1)
-        weave()
-        mix(last, 0, 2)
-        weave()
-        quant_b(last, 3, 1)
-        mixed.extend(range(n - 3, n))
-        mm_u(last, 2, 1)
-        mm_u(last, 3, 1, "acc")
+        mm_u(last, tag="acc")
+        silu(last - 1)
+        silu(last)
+        mixed.extend(range(n - 5, n + 1))
         while small:
+            for m in weighed[:2]:
+                join(m)
+            weighed[:] = weighed[2:]
             weave()
-        silu(last, 2, 1)
         squashes.pop()()
-        silu(last, 3, 1)
+        mix(last - 1)
+        mix(last)
         weigh_ready(TILES)
         for m in weighed:
             join(m)
-        store(last, slice(0, 1))
-        for e in range(E):
-            cols = slice((2 + e) * F, (3 + e) * F)
-            nc.vector.scalar_tensor_tensor(
-                out=q[last][:, cols], in0=pps[last][:, cols], scalar=gate[:, n, e : e + 1], in1=sil[last][:, cols], op0=ALU.mult, op1=ALU.mult
-            )
-        nc.vector.tensor_tensor(out=res[last][:, 1, :], in0=q[last][:, 2 * F : 3 * F], in1=q[last][:, 3 * F : 4 * F], op=ALU.add)
-        store(last, slice(1, 2))

@@ -21,7 +21,8 @@ ALU = mybir.AluOpType
 
 SQRT_SEED = 532487669.0
 GROUPS = (6, 6, 4)
-TURN_AHEAD = 6
+TURN_AHEAD = 4
+SCALE_AHEAD = 7
 JOINS = 3
 
 
@@ -33,7 +34,7 @@ def tile_autonomyofexpertsnormgate_t_kernel(tc, x_bytes, x_scale, wdown, rgain, 
         psum = ctx.enter_context(tc.psum_pool(name="psum", bufs=1))
         ctx.enter_context(tc.manual_schedule())
 
-        xscale = keep.tile([P, 2 * D], F32, name="xscale")
+        xscale = keep.tile([P, D], F32, name="xscale")
         xb, wraw = {}, {}
 
         def load_x(k):
@@ -48,56 +49,43 @@ def tile_autonomyofexpertsnormgate_t_kernel(tc, x_bytes, x_scale, wdown, rgain, 
         nc.sync.dma_start(out=sraw[:, :, 0:4], in_=x_scale.rearrange("o (g p t) -> p (o g) t", g=2, t=4))
         graw = keep.tile([P, E, 16], BF16, name="graw")
         nc.sync.dma_start(out=graw[:, :, 0:4], in_=rgain.rearrange("e (p t) -> p e t", t=4))
-        xb[0] = keep.tile([P, 2, D], U8, name="xb0")
-        for m in range(2):
-            nc.sync.dma_start(out=xb[0][:, m, :], in_=x_bytes[0:256, :].rearrange("(p m) d -> p m d", m=2)[:, m, :])
         load_w(0, 0)
-        load_x(1)
+        load_x(0)
         load_w(0, 1)
         load_w(1, 0)
-        load_x(2)
+        load_x(1)
         load_w(1, 1)
+        load_x(2)
         load_x(3)
-        load_x(4)
         praw = keep.tile([P, E, 2, 4, F], BF16, name="praw")
         for e in range(E):
             nc.sync.dma_start(out=praw[:, e], in_=wp[e].rearrange("(g p j) f -> p g j f", g=2, j=4))
         uraw = keep.tile([P, E, 4, F], BF16, name="uraw")
         nc.sync.dma_start(out=uraw[:], in_=wup.rearrange("e (p j) f -> p e j f", j=4))
-        for k in range(5, PAIRS):
+        for k in range(4, PAIRS):
             load_x(k)
 
         ident = keep.tile([P, P], F32, name="ident")
         make_identity(nc, ident[:])
-        ident16 = keep.tile([P, P], BF16, name="ident16")
-        make_identity(nc, ident16[:])
 
         def spread(column, place):
             nc.tensor.transpose(place, column.to_broadcast([P, P]), ident[:])
 
-        turned = {}
         for g in range(2):
-            turned[g] = psum.tile([P, 4, P], F32, name=("xt", "bt")[g])
+            turned = psum.tile([P, 4, P], F32, name=("xt", "bt")[g])
             for t in range(4):
-                spread(sraw[:, g, t : t + 1], turned[g][:, t, :])
-        for m in range(2):
-            for g in range(2):
-                dst = xscale[:, D * m + 512 * g : D * m + 512 * (g + 1)].rearrange("q (p t) -> q p t", t=4)
-                nc.scalar.copy(out=dst, in_=turned[g][:].rearrange("q t p -> q p t"))
+                spread(sraw[:, g, t : t + 1], turned[:, t, :])
+            dst = xscale[:, 512 * g : 512 * (g + 1)].rearrange("q (p t) -> q p t", t=4)
+            nc.scalar.copy(out=dst, in_=turned[:].rearrange("q t p -> q p t"))
 
         wgrp, wcode, wscale = {}, {}, {}
 
-        def interleave(dst, sources, tag):
-            laid = psum.tile([P, 1024], BF16, name=tag)
-            for h in range(2):
-                nc.tensor.matmul(laid[:, 512 * h : 512 * (h + 1)], lhsT=ident16[:], rhs=sources[h], start=True, stop=True)
-            nc.scalar.copy(out=dst, in_=laid[:])
-
-        def group_w(e, g):
-            wgrp[e, g] = stage.tile([P, 4 * R], BF16, align_bytes=64, name="wgrp", bufs=2)
-            src = wraw[e, g][:].rearrange("q j (p u i) -> q u p i j", u=2, i=2)
-            for u in range(2):
-                interleave(wgrp[e, g][:, 1024 * u : 1024 * (u + 1)], [src[:, u, 0:64], src[:, u, 64:128]], ("uu", "pp")[u])
+        def group_w(e, g, copy):
+            wgrp[e, g] = stage.tile([P, 4 * R], BF16, align_bytes=64, name="wgrp", bufs=3)
+            copy(
+                out=wgrp[e, g][:].rearrange("q (u p i j) -> q p j u i", u=2, i=2, j=4),
+                in_=wraw[e, g][:].rearrange("q j (p u i) -> q p j u i", u=2, i=2),
+            )
 
         def quant_w(e, g):
             wcode[e, g] = keep.tile([P, R], U32, align_bytes=64, name="wcode%d%d" % (e, g))
@@ -107,7 +95,7 @@ def tile_autonomyofexpertsnormgate_t_kernel(tc, x_bytes, x_scale, wdown, rgain, 
         gain = keep.tile([P, E * R], BF16, name="gain")
 
         def spread_gain():
-            spread_words = psum.tile([P, E, 2, P], F32, name="xt")
+            spread_words = psum.tile([P, E, 2, P], F32, name="pp")
             words = graw[:].bitcast(F32)
             for e in range(E):
                 for u in range(2):
@@ -122,10 +110,16 @@ def tile_autonomyofexpertsnormgate_t_kernel(tc, x_bytes, x_scale, wdown, rgain, 
         uscale = keep.tile([P, E * F], U8, align_bytes=64, name="uscale")
 
         def group_p(g):
-            interleave(pgrp[:, 1024 * g : 1024 * (g + 1)], [praw[:, e, g].rearrange("q j f -> q f j") for e in range(E)], ("uu", "pp")[g])
+            nc.scalar.copy(
+                out=pgrp[:, 1024 * g : 1024 * (g + 1)].rearrange("q (e c i j) -> q e c j i", e=E, i=4, j=4),
+                in_=praw[:, :, g].rearrange("q e j (c i) -> q e c j i", i=4),
+            )
 
         def group_u():
-            interleave(ugrp[:], [uraw[:, e].rearrange("q j f -> q f j") for e in range(E)], "uu")
+            nc.scalar.copy(
+                out=ugrp[:].rearrange("q (e c i j) -> q e c j i", e=E, i=4, j=4),
+                in_=uraw[:].rearrange("q e j (c i) -> q e c j i", i=4),
+            )
 
         def quant_p():
             nc.vector.quantize_mx(out=pcode[:].bitcast(X4), scales=pscale[:], in_=pgrp[:])
@@ -139,18 +133,13 @@ def tile_autonomyofexpertsnormgate_t_kernel(tc, x_bytes, x_scale, wdown, rgain, 
         sumsq = keep.tile([P, TILES * E], F32, name="sumsq")
         gate = keep.tile([P, TILES, E], F32, name="gate")
 
-        def scale_x(k):
-            xs[k] = stage.tile([P, 2 * D], BF16, align_bytes=64, name="xs", bufs=5)
-            if k == 0:
-                for m, cols in ((0, slice(0, 512)), (0, slice(512, D)), (1, slice(0, D))):
-                    dst = xs[k][:, D * m + cols.start : D * m + cols.stop]
-                    nc.vector.tensor_tensor(out=dst, in0=xb[k][:, m, cols].bitcast(F8), in1=xscale[:, cols], op=ALU.mult)
-                return
-            nc.vector.tensor_tensor(out=xs[k][:], in0=xb[k][:].rearrange("q m d -> q (m d)").bitcast(F8), in1=xscale[:], op=ALU.mult)
+        def scale_x(n):
+            xs[n] = stage.tile([P, D], BF16, align_bytes=64, name="xs", bufs=6)
+            nc.vector.tensor_tensor(out=xs[n][:], in0=xb[n // 2][:, n % 2, :].bitcast(F8), in1=xscale[:], op=ALU.mult)
 
         def turn_x(n, tag="xt"):
             xt[n] = psum.tile([P, 2, 2, P], F32, name=tag)
-            words = xs[n // 2][:, D * (n % 2) : D * (n % 2 + 1)].bitcast(F32)
+            words = xs[n][:].bitcast(F32)
             for g in range(2):
                 for u in range(2):
                     nc.tensor.transpose(xt[n][:, g, u, :], words[:, 256 * g + u : 256 * (g + 1) : 2], ident[:])
@@ -326,46 +315,38 @@ def tile_autonomyofexpertsnormgate_t_kernel(tc, x_bytes, x_scale, wdown, rgain, 
 
             return [start] + [recip, divide, average] * 3 + [subtract]
 
-        scaled = []
-
-        def scale_next():
-            scale_x(len(scaled))
-            scaled.append(True)
-
         def turn_pair(k):
             turn_x(2 * k)
             turn_x(2 * k + 1, "bt")
             leave_x(2 * k)
             leave_x(2 * k + 1)
 
-        scale_next()
-        scale_next()
-        group_w(0, 0)
-        turn_pair(0)
-        group_w(0, 1)
-        quant_w(0, 0)
-        quant_x(0)
-        group_w(1, 0)
-        quant_w(0, 1)
-        turn_pair(1)
+        group_w(0, 0, nc.vector.tensor_copy)
         spread_gain()
-        scale_next()
-        group_w(1, 1)
-        quant_w(1, 0)
-        quant_x(1)
+        scale_x(0)
+        scale_x(1)
+        group_w(0, 1, nc.scalar.copy)
+        turn_pair(0)
+        quant_w(0, 0)
+        group_w(1, 0, nc.vector.tensor_copy)
+        quant_w(0, 1)
+        quant_x(0)
+        group_w(1, 1, nc.scalar.copy)
         for n in range(2):
             for e in range(E):
                 acc[n, e] = bank("acc")
         for n in range(2):
             mm_a(n, 0)
+        quant_w(1, 0)
+        scale_x(2)
         square(0, 0)
-        turn_pair(2)
-        scale_next()
         quant_w(1, 1)
         for n in range(2):
             mm_a(n, 1)
         square(0, 1)
-        scale_next()
+        scale_x(3)
+        turn_pair(1)
+        scale_x(4)
 
         small, fresh, squashes, gated, mixed, weighed = [], [], [], [], [], []
         ends, total = {}, 0
@@ -385,7 +366,7 @@ def tile_autonomyofexpertsnormgate_t_kernel(tc, x_bytes, x_scale, wdown, rgain, 
                     weigh(gated.pop(0))
 
         for s in range(TILES - 1):
-            joins = weighed[:JOINS] if len(scaled) == PAIRS else []
+            joins = weighed[:JOINS] if s >= TILES - SCALE_AHEAD else []
             weighed[:] = weighed[len(joins) :]
             gain_b(s, 0)
             weave()
@@ -412,30 +393,38 @@ def tile_autonomyofexpertsnormgate_t_kernel(tc, x_bytes, x_scale, wdown, rgain, 
                 weigh_ready(3)
             if s == 0:
                 group_u()
-                group_p(1)
-            if s == 1:
-                group_p(0)
-                quant_u()
+            if s in (1, 2):
+                group_p(s - 1)
             if s == 2:
-                quant_p()
+                quant_u()
+
             if s % 2 == 1 and s >= 3:
                 quant_b((s - 3) // 2)
             if s % 2 == 1 and s >= 5:
                 weave()
                 mix((s - 5) // 2)
                 mixed.extend((s - 5, s - 4))
-            if s % 2 == 0 and (s + 4) // 2 < PAIRS:
-                quant_x((s + 4) // 2)
+            if s == 0:
+                scale_x(TURN_AHEAD + 1)
+                quant_x(1)
             weave()
             if s + 2 < TILES:
                 for e in range(E):
                     mm_a(s + 2, e)
+            if s == 3:
+                quant_p()
             if s % 2 == 1 and s >= 3:
                 mm_u((s - 3) // 2)
                 mm_p((s - 3) // 2)
-            if s % 2 == 1 and len(scaled) < PAIRS:
-                scale_next()
+            if s == 1:
+                scale_x(SCALE_AHEAD)
+            if 1 <= s < TILES - SCALE_AHEAD:
+                scale_x(s + SCALE_AHEAD)
                 weave()
+            elif s == 0:
+                scale_x(TURN_AHEAD + 2)
+            if s % 2 == 1 and (s + 3) // 2 < PAIRS:
+                quant_x((s + 3) // 2)
             for n in joins:
                 join(n)
             if joins:

@@ -20,10 +20,10 @@ ACT = mybir.ActivationFunctionType
 ALU = mybir.AluOpType
 
 SQRT_SEED = 532487669.0
-GROUPS = (6, 6, 4)
+GROUPS = (11, 5)
 TURN_AHEAD = 4
-SCALE_AHEAD = 7
-JOINS = 3
+SCALE_AHEAD = 5
+JOINS = 4
 
 
 def tile_autonomyofexpertsnormgate_t_kernel(tc, x_bytes, x_scale, wdown, rgain, wup, wp, out):
@@ -55,14 +55,12 @@ def tile_autonomyofexpertsnormgate_t_kernel(tc, x_bytes, x_scale, wdown, rgain, 
         load_w(1, 0)
         load_x(1)
         load_w(1, 1)
-        load_x(2)
-        load_x(3)
         praw = keep.tile([P, E, 2, 4, F], BF16, name="praw")
         for e in range(E):
             nc.sync.dma_start(out=praw[:, e], in_=wp[e].rearrange("(g p j) f -> p g j f", g=2, j=4))
         uraw = keep.tile([P, E, 4, F], BF16, name="uraw")
         nc.sync.dma_start(out=uraw[:], in_=wup.rearrange("e (p j) f -> p e j f", j=4))
-        for k in range(4, PAIRS):
+        for k in range(2, PAIRS):
             load_x(k)
 
         ident = keep.tile([P, P], F32, name="ident")
@@ -251,12 +249,12 @@ def tile_autonomyofexpertsnormgate_t_kernel(tc, x_bytes, x_scale, wdown, rgain, 
         def mix(k, first=0, count=4):
             cols = slice(F * first, F * (first + count))
             if first == 0:
-                q[k] = stage.tile([P, 4 * F], F32, name="q", bufs=13)
+                q[k] = stage.tile([P, 4 * F], F32, name="q", bufs=16)
             nc.vector.tensor_tensor(out=q[k][:, cols], in0=sil[k][:, cols], in1=pps[k][:, cols], op=ALU.mult)
 
         def weigh(n):
             k, m = n // 2, n % 2
-            z[n] = stage.tile([P, F], F32, name="z", bufs=24)
+            z[n] = stage.tile([P, F], F32, name="z", bufs=26)
             nc.scalar.activation(out=z[n][:], in_=q[k][:, (2 * m + 1) * F : (2 * m + 2) * F], func=ACT.Copy, scale=gate[:, n, 1:2])
 
         def store(k, ms):
@@ -331,16 +329,18 @@ def tile_autonomyofexpertsnormgate_t_kernel(tc, x_bytes, x_scale, wdown, rgain, 
         group_w(1, 0, nc.vector.tensor_copy)
         quant_w(0, 1)
         quant_x(0)
-        group_w(1, 1, nc.scalar.copy)
+        group_u()
+        group_p(0)
+        group_w(1, 1, nc.vector.tensor_copy)
         for n in range(2):
             for e in range(E):
                 acc[n, e] = bank("acc")
         for n in range(2):
             mm_a(n, 0)
         quant_w(1, 0)
-        scale_x(2)
         square(0, 0)
         quant_w(1, 1)
+        scale_x(2)
         for n in range(2):
             mm_a(n, 1)
         square(0, 1)
@@ -366,7 +366,7 @@ def tile_autonomyofexpertsnormgate_t_kernel(tc, x_bytes, x_scale, wdown, rgain, 
                     weigh(gated.pop(0))
 
         for s in range(TILES - 1):
-            joins = weighed[:JOINS] if s >= TILES - SCALE_AHEAD else []
+            joins = weighed[:JOINS] if TILES - SCALE_AHEAD <= s < TILES - 2 else []
             weighed[:] = weighed[len(joins) :]
             gain_b(s, 0)
             weave()
@@ -392,9 +392,7 @@ def tile_autonomyofexpertsnormgate_t_kernel(tc, x_bytes, x_scale, wdown, rgain, 
             else:
                 weigh_ready(3)
             if s == 0:
-                group_u()
-            if s in (1, 2):
-                group_p(s - 1)
+                group_p(1)
             if s == 2:
                 quant_u()
 
@@ -405,7 +403,6 @@ def tile_autonomyofexpertsnormgate_t_kernel(tc, x_bytes, x_scale, wdown, rgain, 
                 mix((s - 5) // 2)
                 mixed.extend((s - 5, s - 4))
             if s == 0:
-                scale_x(TURN_AHEAD + 1)
                 quant_x(1)
             weave()
             if s + 2 < TILES:
@@ -416,21 +413,23 @@ def tile_autonomyofexpertsnormgate_t_kernel(tc, x_bytes, x_scale, wdown, rgain, 
             if s % 2 == 1 and s >= 3:
                 mm_u((s - 3) // 2)
                 mm_p((s - 3) // 2)
-            if s == 1:
-                scale_x(SCALE_AHEAD)
-            if 1 <= s < TILES - SCALE_AHEAD:
+            if s < TILES - SCALE_AHEAD:
                 scale_x(s + SCALE_AHEAD)
                 weave()
-            elif s == 0:
-                scale_x(TURN_AHEAD + 2)
-            if s % 2 == 1 and (s + 3) // 2 < PAIRS:
-                quant_x((s + 3) // 2)
             for n in joins:
                 join(n)
+            if s % 2 == 1 and (s + 3) // 2 < PAIRS:
+                quant_x((s + 3) // 2)
             if joins:
                 weave()
             small.extend(fresh)
             fresh.clear()
+
+        def fill():
+            for m in weighed[:2]:
+                join(m)
+            weighed[:] = weighed[2:]
+            weave()
 
         n = TILES - 1
         gain_b(n, 0)
@@ -443,6 +442,8 @@ def tile_autonomyofexpertsnormgate_t_kernel(tc, x_bytes, x_scale, wdown, rgain, 
         weave()
         turn_b(n)
         leave_b(n)
+        for i in range(2):
+            fill()
         mix(last - 2)
         weave()
         quant_b(last - 1)
@@ -457,10 +458,7 @@ def tile_autonomyofexpertsnormgate_t_kernel(tc, x_bytes, x_scale, wdown, rgain, 
         silu(last)
         mixed.extend(range(n - 5, n + 1))
         while small:
-            for m in weighed[:2]:
-                join(m)
-            weighed[:] = weighed[2:]
-            weave()
+            fill()
         squashes.pop()()
         mix(last - 1)
         mix(last)

@@ -22,7 +22,7 @@ ALU = mybir.AluOpType
 SQRT_SEED = 532487669.0
 GROUPS = (11, 5)
 TURN_AHEAD = 4
-SCALE_AHEAD = 5
+SCALE_AHEAD = 6
 JOINS = 4
 
 
@@ -379,14 +379,12 @@ def tile_autonomyofexpertsnormgate_t_kernel(tc, x_bytes, x_scale, wdown, rgain, 
                 fresh.extend(gate_steps(*ends[s + 1]))
             if s % 2 == 0 and s >= 4:
                 silu((s - 4) // 2)
-            if s + TURN_AHEAD < TILES:
-                turn_x(s + TURN_AHEAD)
-            if s >= 1:
-                turn_b(s - 1)
-            if s + TURN_AHEAD < TILES:
-                leave_x(s + TURN_AHEAD)
-            if s >= 1:
-                leave_b(s - 1)
+            turns = [(turn_x, leave_x, s + TURN_AHEAD), (turn_b, leave_b, s - 1)]
+            turns = [item for item in turns[:: 2 * (s % 2) - 1] if 0 <= item[2] < TILES]
+            for turn, leave, n in turns:
+                turn(n)
+            for turn, leave, n in turns:
+                leave(n)
             if squashes:
                 squashes.pop(0)()
             else:
@@ -404,6 +402,7 @@ def tile_autonomyofexpertsnormgate_t_kernel(tc, x_bytes, x_scale, wdown, rgain, 
                 mixed.extend((s - 5, s - 4))
             if s == 0:
                 quant_x(1)
+                scale_x(SCALE_AHEAD - 1)
             weave()
             if s + 2 < TILES:
                 for e in range(E):
@@ -411,8 +410,8 @@ def tile_autonomyofexpertsnormgate_t_kernel(tc, x_bytes, x_scale, wdown, rgain, 
             if s == 3:
                 quant_p()
             if s % 2 == 1 and s >= 3:
-                mm_u((s - 3) // 2)
                 mm_p((s - 3) // 2)
+                mm_u((s - 3) // 2)
             if s < TILES - SCALE_AHEAD:
                 scale_x(s + SCALE_AHEAD)
                 weave()

@@ -49,22 +49,27 @@ def tile_autonomyofexpertsnormgate_t_kernel(tc, x_bytes, x_scale, wdown, rgain, 
         nc.sync.dma_start(out=sraw[:, :, 0:4], in_=x_scale.rearrange("o (g p t) -> p (o g) t", g=2, t=4))
         graw = keep.tile([P, E, 16], BF16, name="graw")
         nc.sync.dma_start(out=graw[:, :, 0:4], in_=rgain.rearrange("e (p t) -> p e t", t=4))
-        load_w(0, 0)
+        first_w = {}
+        for h in range(2):
+            first_w[h] = keep.tile([P, 4, R // 2], BF16, name="first_w%d" % h)
+            nc.sync.dma_start(out=first_w[h][:], in_=wdown[0, 0:512, 256 * h : 256 * (h + 1)].rearrange("(p j) c -> p j c", j=4))
         load_x(0)
         load_w(0, 1)
         load_w(1, 0)
+        uraw = keep.tile([P, E, 4, F], BF16, name="uraw")
+        nc.sync.dma_start(out=uraw[:], in_=wup.rearrange("e (p j) f -> p e j f", j=4))
         load_x(1)
         load_w(1, 1)
         praw = keep.tile([P, E, 2, 4, F], BF16, name="praw")
         for e in range(E):
             nc.sync.dma_start(out=praw[:, e], in_=wp[e].rearrange("(g p j) f -> p g j f", g=2, j=4))
-        uraw = keep.tile([P, E, 4, F], BF16, name="uraw")
-        nc.sync.dma_start(out=uraw[:], in_=wup.rearrange("e (p j) f -> p e j f", j=4))
         for k in range(2, PAIRS):
             load_x(k)
 
         ident = keep.tile([P, P], F32, name="ident")
         make_identity(nc, ident[:])
+        ident16 = keep.tile([P, P], BF16, name="ident16")
+        make_identity(nc, ident16[:])
 
         def spread(column, place):
             nc.tensor.transpose(place, column.to_broadcast([P, P]), ident[:])
@@ -84,6 +89,14 @@ def tile_autonomyofexpertsnormgate_t_kernel(tc, x_bytes, x_scale, wdown, rgain, 
                 out=wgrp[e, g][:].rearrange("q (u p i j) -> q p j u i", u=2, i=2, j=4),
                 in_=wraw[e, g][:].rearrange("q j (p u i) -> q p j u i", u=2, i=2),
             )
+
+        def group_first_w():
+            wgrp[0, 0] = stage.tile([P, 4 * R], BF16, align_bytes=64, name="wgrp", bufs=3)
+            for h in range(2):
+                nc.vector.tensor_copy(
+                    out=wgrp[0, 0][:].rearrange("q (u p i j) -> q p j u i", u=2, i=2, j=4)[:, 64 * h : 64 * (h + 1)],
+                    in_=first_w[h][:].rearrange("q j (p u i) -> q p j u i", u=2, i=2),
+                )
 
         def quant_w(e, g):
             wcode[e, g] = keep.tile([P, R], U32, align_bytes=64, name="wcode%d%d" % (e, g))
@@ -107,17 +120,17 @@ def tile_autonomyofexpertsnormgate_t_kernel(tc, x_bytes, x_scale, wdown, rgain, 
         ucode = keep.tile([P, E * F], U32, align_bytes=64, name="ucode")
         uscale = keep.tile([P, E * F], U8, align_bytes=64, name="uscale")
 
+        def interleave(dst, sources, tag):
+            laid = psum.tile([P, 1024], BF16, name=tag)
+            for h in range(2):
+                nc.tensor.matmul(laid[:, 512 * h : 512 * (h + 1)], lhsT=ident16[:], rhs=sources[h], start=True, stop=True)
+            nc.scalar.copy(out=dst, in_=laid[:])
+
         def group_p(g):
-            nc.scalar.copy(
-                out=pgrp[:, 1024 * g : 1024 * (g + 1)].rearrange("q (e c i j) -> q e c j i", e=E, i=4, j=4),
-                in_=praw[:, :, g].rearrange("q e j (c i) -> q e c j i", i=4),
-            )
+            interleave(pgrp[:, 1024 * g : 1024 * (g + 1)], [praw[:, e, g].rearrange("q j f -> q f j") for e in range(E)], ("pp", "uu")[g])
 
         def group_u():
-            nc.scalar.copy(
-                out=ugrp[:].rearrange("q (e c i j) -> q e c j i", e=E, i=4, j=4),
-                in_=uraw[:].rearrange("q e j (c i) -> q e c j i", i=4),
-            )
+            interleave(ugrp[:], [uraw[:, e].rearrange("q j f -> q f j") for e in range(E)], "uu")
 
         def quant_p():
             nc.vector.quantize_mx(out=pcode[:].bitcast(X4), scales=pscale[:], in_=pgrp[:])
@@ -133,7 +146,8 @@ def tile_autonomyofexpertsnormgate_t_kernel(tc, x_bytes, x_scale, wdown, rgain, 
 
         def scale_x(n):
             xs[n] = stage.tile([P, D], BF16, align_bytes=64, name="xs", bufs=6)
-            nc.vector.tensor_tensor(out=xs[n][:], in0=xb[n // 2][:, n % 2, :].bitcast(F8), in1=xscale[:], op=ALU.mult)
+            for cols in (slice(0, 512), slice(512, D)) if n == 0 else (slice(0, D),):
+                nc.vector.tensor_tensor(out=xs[n][:, cols], in0=xb[n // 2][:, n % 2, cols].bitcast(F8), in1=xscale[:, cols], op=ALU.mult)
 
         def turn_x(n, tag="xt"):
             xt[n] = psum.tile([P, 2, 2, P], F32, name=tag)
@@ -319,7 +333,7 @@ def tile_autonomyofexpertsnormgate_t_kernel(tc, x_bytes, x_scale, wdown, rgain, 
             leave_x(2 * k)
             leave_x(2 * k + 1)
 
-        group_w(0, 0, nc.vector.tensor_copy)
+        group_first_w()
         spread_gain()
         scale_x(0)
         scale_x(1)
@@ -329,23 +343,26 @@ def tile_autonomyofexpertsnormgate_t_kernel(tc, x_bytes, x_scale, wdown, rgain, 
         group_w(1, 0, nc.vector.tensor_copy)
         quant_w(0, 1)
         quant_x(0)
+        group_w(1, 1, nc.scalar.copy)
         group_u()
-        group_p(0)
-        group_w(1, 1, nc.vector.tensor_copy)
         for n in range(2):
             for e in range(E):
                 acc[n, e] = bank("acc")
         for n in range(2):
             mm_a(n, 0)
         quant_w(1, 0)
-        square(0, 0)
-        quant_w(1, 1)
         scale_x(2)
+        square(0, 0)
+        turn_x(2)
+        leave_x(2)
+        quant_w(1, 1)
+        scale_x(3)
         for n in range(2):
             mm_a(n, 1)
         square(0, 1)
-        scale_x(3)
-        turn_pair(1)
+        turn_x(3, "bt")
+        leave_x(3)
+        group_p(0)
         scale_x(4)
 
         small, fresh, squashes, gated, mixed, weighed = [], [], [], [], [], []

@@ -23,6 +23,7 @@ SQRT_SEED = 532487669.0
 GROUPS = (11, 5)
 TURN_AHEAD = 4
 SCALE_AHEAD = 6
+SHARES = (352, 160)
 JOINS = 4
 
 
@@ -138,16 +139,27 @@ def tile_autonomyofexpertsnormgate_t_kernel(tc, x_bytes, x_scale, wdown, rgain, 
         def quant_u():
             nc.vector.quantize_mx(out=ucode[:].bitcast(X4), scales=uscale[:], in_=ugrp[:])
 
-        xs, xt, xg, xc, xsc = {}, {}, {}, {}, {}
+        xs, xw, xt, xg, xc, xsc = {}, {}, {}, {}, {}, {}
         acc, bb, bt, bg, bc, bsc = {}, {}, {}, {}, {}, {}
         pps, ups, sil, q, z, res = {}, {}, {}, {}, {}, {}
         sumsq = keep.tile([P, TILES * E], F32, name="sumsq")
         gate = keep.tile([P, TILES, E], F32, name="gate")
 
-        def scale_x(n):
+        def scale_x(n, count=D):
             xs[n] = stage.tile([P, D], BF16, align_bytes=64, name="xs", bufs=6)
-            for cols in (slice(0, 512), slice(512, D)) if n == 0 else (slice(0, D),):
+            for cols in (slice(0, 512), slice(512, D)) if n == 0 else (slice(0, count),):
                 nc.vector.tensor_tensor(out=xs[n][:, cols], in0=xb[n // 2][:, n % 2, cols].bitcast(F8), in1=xscale[:, cols], op=ALU.mult)
+
+        def widen_x(n, start, stop):
+            xw[n, start] = keep.tile([P, stop - start], BF16, name="xw%d_%d" % (n, start))
+            nc.scalar.copy(out=xw[n, start][:, 0 : stop - start - 32], in_=xb[n // 2][:, n % 2, start : stop - 32].bitcast(F8))
+
+        def share_x(n, start, stop):
+            count = stop - start
+            if start == 0:
+                xs[n] = stage.tile([P, D], BF16, align_bytes=64, name="xsg", bufs=2)
+            nc.vector.tensor_copy(out=xw[n, start][:, count - 32 : count], in_=xb[n // 2][:, n % 2, stop - 32 : stop].bitcast(F8))
+            nc.gpsimd.tensor_tensor(out=xs[n][:, start:stop], in0=xw[n, start][:, 0:count], in1=xscale[:, start:stop], op=ALU.mult)
 
         def turn_x(n, tag="xt"):
             xt[n] = psum.tile([P, 2, 2, P], F32, name=tag)
@@ -278,7 +290,7 @@ def tile_autonomyofexpertsnormgate_t_kernel(tc, x_bytes, x_scale, wdown, rgain, 
         def join(n):
             k, m = n // 2, n % 2
             if m == 0:
-                res[k] = stage.tile([P, 2, F], F32, name="res", bufs=6)
+                res[k] = stage.tile([P, 2, F], F32, name="res", bufs=8)
             nc.vector.scalar_tensor_tensor(
                 out=res[k][:, m, :],
                 in0=q[k][:, 2 * m * F : (2 * m + 1) * F],
@@ -371,6 +383,13 @@ def tile_autonomyofexpertsnormgate_t_kernel(tc, x_bytes, x_scale, wdown, rgain, 
             ends[2 * (total + count) - 1] = (total, count)
             total += count
         last = PAIRS - 1
+        shared = range(12, TILES, 4)
+        pieces = {}
+        for n in shared:
+            start = 0
+            for s in range(n - SCALE_AHEAD - 3, n - SCALE_AHEAD + 1):
+                pieces[s] = (n, start, start + SHARES[s % 2])
+                start += SHARES[s % 2]
 
         def weave():
             if small:
@@ -386,12 +405,12 @@ def tile_autonomyofexpertsnormgate_t_kernel(tc, x_bytes, x_scale, wdown, rgain, 
             joins = weighed[:JOINS] if TILES - SCALE_AHEAD <= s < TILES - 2 else []
             weighed[:] = weighed[len(joins) :]
             gain_b(s, 0)
-            weave()
             gain_b(s, 1)
-            weave()
             if s + 1 < TILES:
                 for e in range(E):
                     square(s + 1, e)
+            if s in pieces:
+                widen_x(*pieces[s])
             if s + 1 in ends:
                 fresh.extend(gate_steps(*ends[s + 1]))
             if s % 2 == 0 and s >= 4:
@@ -411,12 +430,12 @@ def tile_autonomyofexpertsnormgate_t_kernel(tc, x_bytes, x_scale, wdown, rgain, 
             if s == 2:
                 quant_u()
 
-            if s % 2 == 1 and s >= 3:
-                quant_b((s - 3) // 2)
             if s % 2 == 1 and s >= 5:
-                weave()
                 mix((s - 5) // 2)
                 mixed.extend((s - 5, s - 4))
+                weave()
+            if s % 2 == 1 and s >= 3:
+                quant_b((s - 3) // 2)
             if s == 0:
                 quant_x(1)
                 scale_x(SCALE_AHEAD - 1)
@@ -427,15 +446,18 @@ def tile_autonomyofexpertsnormgate_t_kernel(tc, x_bytes, x_scale, wdown, rgain, 
             if s == 3:
                 quant_p()
             if s % 2 == 1 and s >= 3:
-                mm_p((s - 3) // 2)
                 mm_u((s - 3) // 2)
-            if s < TILES - SCALE_AHEAD:
-                scale_x(s + SCALE_AHEAD)
-                weave()
+                mm_p((s - 3) // 2)
             for n in joins:
                 join(n)
+            if s < TILES - SCALE_AHEAD and s + SCALE_AHEAD not in shared:
+                scale_x(s + SCALE_AHEAD)
+                weave()
             if s % 2 == 1 and (s + 3) // 2 < PAIRS:
                 quant_x((s + 3) // 2)
+                weave()
+            if s in pieces:
+                share_x(*pieces[s])
             if joins:
                 weave()
             small.extend(fresh)

@@ -20,10 +20,10 @@ ACT = mybir.ActivationFunctionType
 ALU = mybir.AluOpType
 
 SQRT_SEED = 532487669.0
-GROUPS = (11, 5)
+GROUPS = (10, 6)
 TURN_AHEAD = 4
-SCALE_AHEAD = 6
-SHARES = (352, 160)
+SCALE_AHEAD = 7
+OWN = 384
 JOINS = 4
 
 
@@ -35,7 +35,7 @@ def tile_autonomyofexpertsnormgate_t_kernel(tc, x_bytes, x_scale, wdown, rgain, 
         psum = ctx.enter_context(tc.psum_pool(name="psum", bufs=1))
         ctx.enter_context(tc.manual_schedule())
 
-        xscale = keep.tile([P, D], F32, name="xscale")
+        xscale = keep.tile([P, D + OWN], F32, name="xscale")
         xb, wraw = {}, {}
 
         def load_x(k):
@@ -66,6 +66,10 @@ def tile_autonomyofexpertsnormgate_t_kernel(tc, x_bytes, x_scale, wdown, rgain, 
             nc.sync.dma_start(out=praw[:, e], in_=wp[e].rearrange("(g p j) f -> p g j f", g=2, j=4))
         for k in range(2, PAIRS):
             load_x(k)
+
+        idle = keep.tile([P, 1], F32, name="idle")
+        nc.vector.memset(idle[:], 0.0)
+        nc.scalar.activation(out=idle[:], in_=idle[:], func=ACT.Silu)
 
         ident = keep.tile([P, P], F32, name="ident")
         make_identity(nc, ident[:])
@@ -145,28 +149,35 @@ def tile_autonomyofexpertsnormgate_t_kernel(tc, x_bytes, x_scale, wdown, rgain, 
         sumsq = keep.tile([P, TILES * E], F32, name="sumsq")
         gate = keep.tile([P, TILES, E], F32, name="gate")
 
-        def scale_x(n, count=D):
-            xs[n] = stage.tile([P, D], BF16, align_bytes=64, name="xs", bufs=6)
-            for cols in (slice(0, 512), slice(512, D)) if n == 0 else (slice(0, count),):
-                nc.vector.tensor_tensor(out=xs[n][:, cols], in0=xb[n // 2][:, n % 2, cols].bitcast(F8), in1=xscale[:, cols], op=ALU.mult)
+        def scale_x(n, start=0, stop=D):
+            k, base = n // 2, D * (n % 2)
+            if base + start == 0:
+                xs[k] = stage.tile([P, 2 * D], BF16, align_bytes=64, name="xs", bufs=4)
+            codes = xb[k][:].rearrange("q m d -> q (m d)")[:, base + start : base + stop]
+            nc.vector.tensor_tensor(out=xs[k][:, base + start : base + stop], in0=codes.bitcast(F8), in1=xscale[:, start:stop], op=ALU.mult)
 
-        def widen_x(n, start, stop):
-            xw[n, start] = keep.tile([P, stop - start], BF16, name="xw%d_%d" % (n, start))
-            nc.scalar.copy(out=xw[n, start][:, 0 : stop - start - 32], in_=xb[n // 2][:, n % 2, start : stop - 32].bitcast(F8))
+        def widen_x(k):
+            xw[k] = stage.tile([P, D - OWN], BF16, name="xw", bufs=1)
+            nc.scalar.copy(out=xw[k][:, 32:], in_=xb[k][:, 1, OWN + 32 : D].bitcast(F8))
 
-        def share_x(n, start, stop):
-            count = stop - start
-            if start == 0:
-                xs[n] = stage.tile([P, D], BF16, align_bytes=64, name="xsg", bufs=2)
-            nc.vector.tensor_copy(out=xw[n, start][:, count - 32 : count], in_=xb[n // 2][:, n % 2, stop - 32 : stop].bitcast(F8))
-            nc.gpsimd.tensor_tensor(out=xs[n][:, start:stop], in0=xw[n, start][:, 0:count], in1=xscale[:, start:stop], op=ALU.mult)
+        def share_x(k):
+            nc.vector.tensor_copy(out=xw[k][:, 0:32], in_=xb[k][:, 1, OWN : OWN + 32].bitcast(F8))
+            nc.gpsimd.tensor_tensor(out=xs[k][:, D + OWN : D + 512], in0=xw[k][:, 0 : 512 - OWN], in1=xscale[:, OWN:512], op=ALU.mult)
+            nc.gpsimd.tensor_tensor(
+                out=xs[k][:, D + 512 : 2 * D].rearrange("q (u p e) -> q u p e", u=2, e=2),
+                in0=xw[k][:, 512 - OWN :].rearrange("q (p u e) -> q u p e", u=2, e=2),
+                in1=xscale[:, 512:D].rearrange("q (p u e) -> q u p e", u=2, e=2),
+                op=ALU.mult,
+            )
 
         def turn_x(n, tag="xt"):
             xt[n] = psum.tile([P, 2, 2, P], F32, name=tag)
-            words = xs[n][:].bitcast(F32)
+            words = xs[n // 2][:, D * (n % 2) : D * (n % 2 + 1)].bitcast(F32)
             for g in range(2):
                 for u in range(2):
-                    nc.tensor.transpose(xt[n][:, g, u, :], words[:, 256 * g + u : 256 * (g + 1) : 2], ident[:])
+                    apart = g == 1 and n % 2 == 1 and n // 2 in xw
+                    cols = slice(256 + P * u, 256 + P * (u + 1)) if apart else slice(256 * g + u, 256 * (g + 1), 2)
+                    nc.tensor.transpose(xt[n][:, g, u, :], words[:, cols], ident[:])
 
         def leave_x(n):
             k, m = n // 2, n % 2
@@ -278,10 +289,14 @@ def tile_autonomyofexpertsnormgate_t_kernel(tc, x_bytes, x_scale, wdown, rgain, 
                 q[k] = stage.tile([P, 4 * F], F32, name="q", bufs=16)
             nc.vector.tensor_tensor(out=q[k][:, cols], in0=sil[k][:, cols], in1=pps[k][:, cols], op=ALU.mult)
 
-        def weigh(n):
+        def weigh(n, on_scalar):
             k, m = n // 2, n % 2
-            z[n] = stage.tile([P, F], F32, name="z", bufs=26)
-            nc.scalar.activation(out=z[n][:], in_=q[k][:, (2 * m + 1) * F : (2 * m + 2) * F], func=ACT.Copy, scale=gate[:, n, 1:2])
+            z[n] = stage.tile([P, F], F32, name="z", bufs=16)
+            product = q[k][:, (2 * m + 1) * F : (2 * m + 2) * F]
+            if on_scalar:
+                nc.scalar.activation(out=z[n][:], in_=product, func=ACT.Copy, scale=gate[:, n, 1:2])
+            else:
+                nc.vector.tensor_scalar(out=z[n][:], in0=product, scalar1=gate[:, n, 1:2], scalar2=None, op0=ALU.mult)
 
         def store(k, ms):
             rows = out[256 * k : 256 * k + 256, :].rearrange("(p m) f -> p m f", m=2)
@@ -347,7 +362,8 @@ def tile_autonomyofexpertsnormgate_t_kernel(tc, x_bytes, x_scale, wdown, rgain, 
 
         group_first_w()
         spread_gain()
-        scale_x(0)
+        scale_x(0, 0, 512)
+        scale_x(0, 512, D)
         scale_x(1)
         group_w(0, 1, nc.scalar.copy)
         turn_pair(0)
@@ -383,34 +399,27 @@ def tile_autonomyofexpertsnormgate_t_kernel(tc, x_bytes, x_scale, wdown, rgain, 
             ends[2 * (total + count) - 1] = (total, count)
             total += count
         last = PAIRS - 1
-        shared = range(12, TILES, 4)
-        pieces = {}
-        for n in shared:
-            start = 0
-            for s in range(n - SCALE_AHEAD - 3, n - SCALE_AHEAD + 1):
-                pieces[s] = (n, start, start + SHARES[s % 2])
-                start += SHARES[s % 2]
 
         def weave():
             if small:
                 small.pop(0)()
 
-        def weigh_ready(count):
+        def weigh_ready(count, on_scalar):
             for i in range(count):
                 if gated and gated[0] in mixed:
                     weighed.append(gated[0])
-                    weigh(gated.pop(0))
+                    weigh(gated.pop(0), on_scalar)
 
         for s in range(TILES - 1):
-            joins = weighed[:JOINS] if TILES - SCALE_AHEAD <= s < TILES - 2 else []
-            weighed[:] = weighed[len(joins) :]
+            pair = (s + SCALE_AHEAD) // 2 if s % 2 == 1 and s + SCALE_AHEAD < TILES else None
+            before = weighed[:JOINS] if s < TILES - 2 else []
+            weighed[:] = weighed[len(before) :]
             gain_b(s, 0)
             gain_b(s, 1)
-            if s + 1 < TILES:
-                for e in range(E):
-                    square(s + 1, e)
-            if s in pieces:
-                widen_x(*pieces[s])
+            for e in range(E):
+                square(s + 1, e)
+            if pair:
+                widen_x(pair)
             if s + 1 in ends:
                 fresh.extend(gate_steps(*ends[s + 1]))
             if s % 2 == 0 and s >= 4:
@@ -423,23 +432,24 @@ def tile_autonomyofexpertsnormgate_t_kernel(tc, x_bytes, x_scale, wdown, rgain, 
                 leave(n)
             if squashes:
                 squashes.pop(0)()
-            else:
-                weigh_ready(3)
+            elif s >= TILES - TURN_AHEAD:
+                weigh_ready(3, True)
             if s == 0:
                 group_p(1)
-            if s == 2:
+                nc.scalar.copy(out=xscale[:, D : D + OWN], in_=xscale[:, 0:OWN])
+                quant_x(1)
+                scale_x(5)
+                scale_x(6)
+            if s == 1:
                 quant_u()
-
+                scale_x(7)
             if s % 2 == 1 and s >= 5:
                 mix((s - 5) // 2)
                 mixed.extend((s - 5, s - 4))
                 weave()
             if s % 2 == 1 and s >= 3:
                 quant_b((s - 3) // 2)
-            if s == 0:
-                quant_x(1)
-                scale_x(SCALE_AHEAD - 1)
-            weave()
+                weave()
             if s + 2 < TILES:
                 for e in range(E):
                     mm_a(s + 2, e)
@@ -448,18 +458,19 @@ def tile_autonomyofexpertsnormgate_t_kernel(tc, x_bytes, x_scale, wdown, rgain, 
             if s % 2 == 1 and s >= 3:
                 mm_u((s - 3) // 2)
                 mm_p((s - 3) // 2)
-            for n in joins:
-                join(n)
-            if s < TILES - SCALE_AHEAD and s + SCALE_AHEAD not in shared:
-                scale_x(s + SCALE_AHEAD)
+            if s >= TILES - SCALE_AHEAD:
+                for n in before:
+                    join(n)
+                if s < TILES - TURN_AHEAD:
+                    weigh_ready(JOINS, False)
+            if pair:
+                scale_x(2 * pair, 0, D + OWN)
                 weave()
             if s % 2 == 1 and (s + 3) // 2 < PAIRS:
                 quant_x((s + 3) // 2)
                 weave()
-            if s in pieces:
-                share_x(*pieces[s])
-            if joins:
-                weave()
+            if pair:
+                share_x(pair)
             small.extend(fresh)
             fresh.clear()
 
@@ -500,6 +511,6 @@ def tile_autonomyofexpertsnormgate_t_kernel(tc, x_bytes, x_scale, wdown, rgain, 
         squashes.pop()()
         mix(last - 1)
         mix(last)
-        weigh_ready(TILES)
+        weigh_ready(TILES, True)
         for m in weighed:
             join(m)

@@ -23,7 +23,7 @@ SQRT_SEED = 532487669.0
 GROUPS = (10, 6)
 TURN_AHEAD = 4
 SCALE_AHEAD = 7
-OWN = 384
+WIDEN = 448
 JOINS = 4
 
 
@@ -35,7 +35,7 @@ def tile_autonomyofexpertsnormgate_t_kernel(tc, x_bytes, x_scale, wdown, rgain, 
         psum = ctx.enter_context(tc.psum_pool(name="psum", bufs=1))
         ctx.enter_context(tc.manual_schedule())
 
-        xscale = keep.tile([P, D + OWN], F32, name="xscale")
+        xscale = keep.tile([P, D], F32, name="xscale")
         xb, wraw = {}, {}
 
         def load_x(k):
@@ -150,33 +150,31 @@ def tile_autonomyofexpertsnormgate_t_kernel(tc, x_bytes, x_scale, wdown, rgain, 
         gate = keep.tile([P, TILES, E], F32, name="gate")
 
         def scale_x(n, start=0, stop=D):
-            k, base = n // 2, D * (n % 2)
-            if base + start == 0:
-                xs[k] = stage.tile([P, 2 * D], BF16, align_bytes=64, name="xs", bufs=4)
-            codes = xb[k][:].rearrange("q m d -> q (m d)")[:, base + start : base + stop]
-            nc.vector.tensor_tensor(out=xs[k][:, base + start : base + stop], in0=codes.bitcast(F8), in1=xscale[:, start:stop], op=ALU.mult)
+            if start == 0:
+                xs[n] = stage.tile([P, D], BF16, align_bytes=64, name="xs", bufs=5)
+            nc.vector.tensor_tensor(out=xs[n][:, start:stop], in0=xb[n // 2][:, n % 2, start:stop].bitcast(F8), in1=xscale[:, start:stop], op=ALU.mult)
 
-        def widen_x(k):
-            xw[k] = stage.tile([P, D - OWN], BF16, name="xw", bufs=1)
-            nc.scalar.copy(out=xw[k][:, 32:], in_=xb[k][:, 1, OWN + 32 : D].bitcast(F8))
+        def widen_x(n):
+            xw[n] = stage.tile([P, D], BF16, name="xw", bufs=1)
+            nc.scalar.copy(out=xw[n][:, WIDEN:D], in_=xb[n // 2][:, n % 2, WIDEN:D].bitcast(F8))
 
-        def share_x(k):
-            nc.vector.tensor_copy(out=xw[k][:, 0:32], in_=xb[k][:, 1, OWN : OWN + 32].bitcast(F8))
-            nc.gpsimd.tensor_tensor(out=xs[k][:, D + OWN : D + 512], in0=xw[k][:, 0 : 512 - OWN], in1=xscale[:, OWN:512], op=ALU.mult)
+        def share_x(n):
+            nc.vector.tensor_copy(out=xw[n][:, 0:WIDEN], in_=xb[n // 2][:, n % 2, 0:WIDEN].bitcast(F8))
+            xs[n] = stage.tile([P, D], BF16, align_bytes=64, name="xs_apart", bufs=2)
             nc.gpsimd.tensor_tensor(
-                out=xs[k][:, D + 512 : 2 * D].rearrange("q (u p e) -> q u p e", u=2, e=2),
-                in0=xw[k][:, 512 - OWN :].rearrange("q (p u e) -> q u p e", u=2, e=2),
-                in1=xscale[:, 512:D].rearrange("q (p u e) -> q u p e", u=2, e=2),
+                out=xs[n][:].rearrange("q (u c e) -> q u c e", u=2, e=2),
+                in0=xw[n][:].rearrange("q (c u e) -> q u c e", u=2, e=2),
+                in1=xscale[:].rearrange("q (c u e) -> q u c e", u=2, e=2),
                 op=ALU.mult,
             )
 
         def turn_x(n, tag="xt"):
             xt[n] = psum.tile([P, 2, 2, P], F32, name=tag)
-            words = xs[n // 2][:, D * (n % 2) : D * (n % 2 + 1)].bitcast(F32)
+            words = xs[n][:].bitcast(F32)
             for g in range(2):
                 for u in range(2):
-                    apart = g == 1 and n % 2 == 1 and n // 2 in xw
-                    cols = slice(256 + P * u, 256 + P * (u + 1)) if apart else slice(256 * g + u, 256 * (g + 1), 2)
+                    first = 256 * u + P * g
+                    cols = slice(first, first + P) if n in xw else slice(256 * g + u, 256 * (g + 1), 2)
                     nc.tensor.transpose(xt[n][:, g, u, :], words[:, cols], ident[:])
 
         def leave_x(n):
@@ -391,7 +389,11 @@ def tile_autonomyofexpertsnormgate_t_kernel(tc, x_bytes, x_scale, wdown, rgain, 
         turn_x(3, "bt")
         leave_x(3)
         group_p(0)
-        scale_x(4)
+        widen_x(7)
+        for n in (4, 5, 6):
+            scale_x(n)
+        quant_x(1)
+        share_x(7)
 
         small, fresh, squashes, gated, mixed, weighed = [], [], [], [], [], []
         ends, total = {}, 0
@@ -419,7 +421,7 @@ def tile_autonomyofexpertsnormgate_t_kernel(tc, x_bytes, x_scale, wdown, rgain, 
             for e in range(E):
                 square(s + 1, e)
             if pair:
-                widen_x(pair)
+                widen_x(2 * pair + 1)
             if s + 1 in ends:
                 fresh.extend(gate_steps(*ends[s + 1]))
             if s % 2 == 0 and s >= 4:
@@ -436,13 +438,8 @@ def tile_autonomyofexpertsnormgate_t_kernel(tc, x_bytes, x_scale, wdown, rgain, 
                 weigh_ready(3, True)
             if s == 0:
                 group_p(1)
-                nc.scalar.copy(out=xscale[:, D : D + OWN], in_=xscale[:, 0:OWN])
-                quant_x(1)
-                scale_x(5)
-                scale_x(6)
             if s == 1:
                 quant_u()
-                scale_x(7)
             if s % 2 == 1 and s >= 5:
                 mix((s - 5) // 2)
                 mixed.extend((s - 5, s - 4))
@@ -464,13 +461,13 @@ def tile_autonomyofexpertsnormgate_t_kernel(tc, x_bytes, x_scale, wdown, rgain, 
                 if s < TILES - TURN_AHEAD:
                     weigh_ready(JOINS, False)
             if pair:
-                scale_x(2 * pair, 0, D + OWN)
+                scale_x(2 * pair)
                 weave()
             if s % 2 == 1 and (s + 3) // 2 < PAIRS:
                 quant_x((s + 3) // 2)
                 weave()
             if pair:
-                share_x(pair)
+                share_x(2 * pair + 1)
             small.extend(fresh)
             fresh.clear()
 

@@ -21,7 +21,7 @@ ALU = mybir.AluOpType
 
 SQRT_SEED = 532487669.0
 GROUPS = (10, 6)
-TURN_AHEAD = 4
+TURN_AHEAD = 5
 SCALE_AHEAD = 7
 WIDEN = 448
 JOINS = 4
@@ -38,9 +38,12 @@ def tile_autonomyofexpertsnormgate_t_kernel(tc, x_bytes, x_scale, wdown, rgain, 
         xscale = keep.tile([P, D], F32, name="xscale")
         xb, wraw = {}, {}
 
-        def load_x(k):
-            xb[k] = keep.tile([P, 2, D], U8, name="xb%d" % k)
-            nc.sync.dma_start(out=xb[k][:], in_=x_bytes[256 * k : 256 * k + 256, :].rearrange("(p m) d -> p m d", m=2))
+        def load_x(first, count=1):
+            codes = keep.tile([P, count, 2, D], U8, name="xb%d" % first)
+            rows = x_bytes[256 * first : 256 * (first + count), :]
+            nc.sync.dma_start(out=codes[:], in_=rows.rearrange("(k p m) d -> p k m d", k=count, m=2))
+            for k in range(count):
+                xb[first + k] = codes[:, k]
 
         def load_w(e, g):
             wraw[e, g] = keep.tile([P, 4, R], BF16, name="wraw%d%d" % (e, g))
@@ -64,8 +67,10 @@ def tile_autonomyofexpertsnormgate_t_kernel(tc, x_bytes, x_scale, wdown, rgain, 
         praw = keep.tile([P, E, 2, 4, F], BF16, name="praw")
         for e in range(E):
             nc.sync.dma_start(out=praw[:, e], in_=wp[e].rearrange("(g p j) f -> p g j f", g=2, j=4))
-        for k in range(2, PAIRS):
-            load_x(k)
+        load_x(2)
+        load_x(3)
+        for k in range(4, PAIRS, 3):
+            load_x(k, 3)
 
         idle = keep.tile([P, 1], F32, name="idle")
         nc.vector.memset(idle[:], 0.0)
@@ -386,14 +391,17 @@ def tile_autonomyofexpertsnormgate_t_kernel(tc, x_bytes, x_scale, wdown, rgain, 
         for n in range(2):
             mm_a(n, 1)
         square(0, 1)
+        widen_x(7)
         turn_x(3, "bt")
         leave_x(3)
+        scale_x(4)
+        turn_x(4)
+        leave_x(4)
         group_p(0)
-        widen_x(7)
-        for n in (4, 5, 6):
-            scale_x(n)
-        quant_x(1)
+        scale_x(5)
+        scale_x(6)
         share_x(7)
+        quant_x(1)
 
         small, fresh, squashes, gated, mixed, weighed = [], [], [], [], [], []
         ends, total = {}, 0
@@ -417,7 +425,11 @@ def tile_autonomyofexpertsnormgate_t_kernel(tc, x_bytes, x_scale, wdown, rgain, 
             before = weighed[:JOINS] if s < TILES - 2 else []
             weighed[:] = weighed[len(before) :]
             gain_b(s, 0)
+            if s > TILES - SCALE_AHEAD:
+                weave()
             gain_b(s, 1)
+            if s > TILES - SCALE_AHEAD:
+                weave()
             for e in range(E):
                 square(s + 1, e)
             if pair:
@@ -435,7 +447,7 @@ def tile_autonomyofexpertsnormgate_t_kernel(tc, x_bytes, x_scale, wdown, rgain, 
             if squashes:
                 squashes.pop(0)()
             elif s >= TILES - TURN_AHEAD:
-                weigh_ready(3, True)
+                weigh_ready(2, True)
             if s == 0:
                 group_p(1)
             if s == 1:
@@ -458,56 +470,61 @@ def tile_autonomyofexpertsnormgate_t_kernel(tc, x_bytes, x_scale, wdown, rgain, 
             if s >= TILES - SCALE_AHEAD:
                 for n in before:
                     join(n)
-                if s < TILES - TURN_AHEAD:
-                    weigh_ready(JOINS, False)
+                weigh_ready(JOINS if s < TILES - TURN_AHEAD else 1, False)
             if pair:
                 scale_x(2 * pair)
                 weave()
-            if s % 2 == 1 and (s + 3) // 2 < PAIRS:
-                quant_x((s + 3) // 2)
-                weave()
             if pair:
                 share_x(2 * pair + 1)
+            if s % 2 == 1 and (s + 3) // 2 < PAIRS:
+                weave()
+                quant_x((s + 3) // 2)
             small.extend(fresh)
             fresh.clear()
+
+        def tick():
+            weave()
+            if squashes:
+                squashes.pop()()
+            else:
+                weigh_ready(2, True)
 
         def fill():
             for m in weighed[:2]:
                 join(m)
             weighed[:] = weighed[2:]
-            weave()
+            tick()
 
         n = TILES - 1
         gain_b(n, 0)
-        weave()
+        tick()
         turn_b(n - 1, tag="xt")
         leave_b(n - 1)
         mm_p(last - 1, "acc")
-        mm_p(last, "acc")
         gain_b(n, 1)
-        weave()
+        tick()
         turn_b(n)
         leave_b(n)
-        for i in range(2):
-            fill()
+        mm_p(last, "acc")
+        fill()
         mix(last - 2)
-        weave()
+        mixed.extend((n - 5, n - 4))
+        tick()
         quant_b(last - 1)
-        weave()
+        tick()
         mm_u(last - 1)
         quant_b(last, 0, 2)
-        weave()
+        tick()
         quant_b(last, 2, 2)
-        weave()
+        tick()
         mm_u(last, tag="acc")
         silu(last - 1)
         silu(last)
-        mixed.extend(range(n - 5, n + 1))
         while small:
             fill()
-        squashes.pop()()
         mix(last - 1)
         mix(last)
+        mixed.extend(range(n - 3, n + 1))
         weigh_ready(TILES, True)
         for m in weighed:
             join(m)

@@ -20,7 +20,7 @@ ACT = mybir.ActivationFunctionType
 ALU = mybir.AluOpType
 
 SQRT_SEED = 532487669.0
-GROUPS = (10, 6)
+GROUPS = (10, 4, 2)
 TURN_AHEAD = 5
 SCALE_AHEAD = 7
 WIDEN = 448
@@ -294,7 +294,7 @@ def tile_autonomyofexpertsnormgate_t_kernel(tc, x_bytes, x_scale, wdown, rgain, 
 
         def weigh(n, on_scalar):
             k, m = n // 2, n % 2
-            z[n] = stage.tile([P, F], F32, name="z", bufs=16)
+            z[n] = stage.tile([P, F], F32, name="z", bufs=20)
             product = q[k][:, (2 * m + 1) * F : (2 * m + 2) * F]
             if on_scalar:
                 nc.scalar.activation(out=z[n][:], in_=product, func=ACT.Copy, scale=gate[:, n, 1:2])
@@ -394,10 +394,13 @@ def tile_autonomyofexpertsnormgate_t_kernel(tc, x_bytes, x_scale, wdown, rgain, 
         widen_x(7)
         turn_x(3, "bt")
         leave_x(3)
+        for e in range(E):
+            square(1, e)
+        group_p(0)
         scale_x(4)
         turn_x(4)
         leave_x(4)
-        group_p(0)
+        group_p(1)
         scale_x(5)
         scale_x(6)
         share_x(7)
@@ -430,7 +433,7 @@ def tile_autonomyofexpertsnormgate_t_kernel(tc, x_bytes, x_scale, wdown, rgain, 
             gain_b(s, 1)
             if s > TILES - SCALE_AHEAD:
                 weave()
-            for e in range(E):
+            for e in (0, 1) if s % 2 == 1 else (1, 0) if s > 0 else ():
                 square(s + 1, e)
             if pair:
                 widen_x(2 * pair + 1)
@@ -447,9 +450,7 @@ def tile_autonomyofexpertsnormgate_t_kernel(tc, x_bytes, x_scale, wdown, rgain, 
             if squashes:
                 squashes.pop(0)()
             elif s >= TILES - TURN_AHEAD:
-                weigh_ready(2, True)
-            if s == 0:
-                group_p(1)
+                weigh_ready(3, True)
             if s == 1:
                 quant_u()
             if s % 2 == 1 and s >= 5:
@@ -461,6 +462,8 @@ def tile_autonomyofexpertsnormgate_t_kernel(tc, x_bytes, x_scale, wdown, rgain, 
                 weave()
             if s + 2 < TILES:
                 for e in range(E):
+                    acc[s + 2, e] = bank("acc")
+                for e in (1, 0) if s % 2 == 1 else (0, 1):
                     mm_a(s + 2, e)
             if s == 3:
                 quant_p()
@@ -470,11 +473,11 @@ def tile_autonomyofexpertsnormgate_t_kernel(tc, x_bytes, x_scale, wdown, rgain, 
             if s >= TILES - SCALE_AHEAD:
                 for n in before:
                     join(n)
-                weigh_ready(JOINS if s < TILES - TURN_AHEAD else 1, False)
+                if s < TILES - TURN_AHEAD:
+                    weigh_ready(JOINS, False)
             if pair:
                 scale_x(2 * pair)
                 weave()
-            if pair:
                 share_x(2 * pair + 1)
             if s % 2 == 1 and (s + 3) // 2 < PAIRS:
                 weave()

from contextlib import ExitStack

import concourse.mybir as mybir
from concourse.masks import make_identity

T, D, E, R, F = 4096, 1024, 2, 512, 128
P = 128
TILES = T // P
PAIRS = TILES // 2
FLOPS = 2 * T * (D * E * R + D * E * F + E * R * F)

F32 = mybir.dt.float32
BF16 = mybir.dt.bfloat16
I32 = mybir.dt.int32
U32 = mybir.dt.uint32
U8 = mybir.dt.uint8
F8 = mybir.dt.float8_e4m3fn
X4 = mybir.dt.float8_e4m3fn_x4
ACT = mybir.ActivationFunctionType
ALU = mybir.AluOpType

SQRT_SEED = 532487669.0
GROUPS = (10, 4, 2)
TURN_AHEAD = 5
SCALE_AHEAD = 7
WIDEN = 448
JOINS = 4


def tile_autonomyofexpertsnormgate_t_kernel(tc, x_bytes, x_scale, wdown, rgain, wup, wp, out):
    nc = tc.nc
    with ExitStack() as ctx:
        keep = ctx.enter_context(tc.tile_pool(name="keep", bufs=1))
        stage = ctx.enter_context(tc.tile_pool(name="stage", bufs=2))
        psum = ctx.enter_context(tc.psum_pool(name="psum", bufs=1))
        ctx.enter_context(tc.manual_schedule())

        xscale = keep.tile([P, D], F32, name="xscale")
        xb, wraw = {}, {}

        def load_x(first, count=1):
            codes = keep.tile([P, count, 2, D], U8, name="xb%d" % first)
            rows = x_bytes[256 * first : 256 * (first + count), :]
            nc.sync.dma_start(out=codes[:], in_=rows.rearrange("(k p m) d -> p k m d", k=count, m=2))
            for k in range(count):
                xb[first + k] = codes[:, k]

        def load_w(e, g):
            wraw[e, g] = keep.tile([P, 4, R], BF16, name="wraw%d%d" % (e, g))
            nc.sync.dma_start(out=wraw[e, g][:], in_=wdown[e, 512 * g : 512 * g + 512, :].rearrange("(p j) c -> p j c", j=4))

        sraw = keep.tile([P, 2, 8], F32, name="sraw")
        nc.sync.dma_start(out=sraw[:, :, 0:4], in_=x_scale.rearrange("o (g p t) -> p (o g) t", g=2, t=4))
        graw = keep.tile([P, E, 16], BF16, name="graw")
        nc.sync.dma_start(out=graw[:, :, 0:4], in_=rgain.rearrange("e (p t) -> p e t", t=4))
        first_w = {}
        for h in range(2):
            first_w[h] = keep.tile([P, 4, R // 2], BF16, name="first_w%d" % h)
            nc.sync.dma_start(out=first_w[h][:], in_=wdown[0, 0:512, 256 * h : 256 * (h + 1)].rearrange("(p j) c -> p j c", j=4))
        load_x(0)
        load_w(0, 1)
        load_w(1, 0)
        uraw = keep.tile([P, E, 4, F], BF16, name="uraw")
        nc.sync.dma_start(out=uraw[:], in_=wup.rearrange("e (p j) f -> p e j f", j=4))
        load_x(1)
        load_w(1, 1)
        praw = keep.tile([P, E, 2, 4, F], BF16, name="praw")
        for e in range(E):
            nc.sync.dma_start(out=praw[:, e], in_=wp[e].rearrange("(g p j) f -> p g j f", g=2, j=4))
        load_x(2)
        load_x(3)
        for k in range(4, PAIRS, 3):
            load_x(k, 3)

        idle = keep.tile([P, 1], F32, name="idle")
        nc.vector.memset(idle[:], 0.0)
        nc.scalar.activation(out=idle[:], in_=idle[:], func=ACT.Silu)

        ident = keep.tile([P, P], F32, name="ident")
        make_identity(nc, ident[:])
        ident16 = keep.tile([P, P], BF16, name="ident16")
        make_identity(nc, ident16[:])

        def spread(column, place):
            nc.tensor.transpose(place, column.to_broadcast([P, P]), ident[:])

        for g in range(2):
            turned = psum.tile([P, 4, P], F32, name=("xt", "bt")[g])
            for t in range(4):
                spread(sraw[:, g, t : t + 1], turned[:, t, :])
            dst = xscale[:, 512 * g : 512 * (g + 1)].rearrange("q (p t) -> q p t", t=4)
            nc.scalar.copy(out=dst, in_=turned[:].rearrange("q t p -> q p t"))

        wgrp, wcode, wscale = {}, {}, {}

        def group_w(e, g, copy):
            wgrp[e, g] = stage.tile([P, 4 * R], BF16, align_bytes=64, name="wgrp", bufs=3)
            copy(
                out=wgrp[e, g][:].rearrange("q (u p i j) -> q p j u i", u=2, i=2, j=4),
                in_=wraw[e, g][:].rearrange("q j (p u i) -> q p j u i", u=2, i=2),
            )

        def group_first_w():
            wgrp[0, 0] = stage.tile([P, 4 * R], BF16, align_bytes=64, name="wgrp", bufs=3)
            for h in range(2):
                nc.vector.tensor_copy(
                    out=wgrp[0, 0][:].rearrange("q (u p i j) -> q p j u i", u=2, i=2, j=4)[:, 64 * h : 64 * (h + 1)],
                    in_=first_w[h][:].rearrange("q j (p u i) -> q p j u i", u=2, i=2),
                )

        def quant_w(e, g):
            wcode[e, g] = keep.tile([P, R], U32, align_bytes=64, name="wcode%d%d" % (e, g))
            wscale[e, g] = keep.tile([P, R], U8, align_bytes=64, name="wscale%d%d" % (e, g))
            nc.vector.quantize_mx(out=wcode[e, g][:].bitcast(X4), scales=wscale[e, g][:], in_=wgrp[e, g][:])

        gain = keep.tile([P, E * R], BF16, name="gain")

        def spread_gain():
            spread_words = psum.tile([P, E, 2, P], F32, name="pp")
            words = graw[:].bitcast(F32)
            for e in range(E):
                for u in range(2):
                    spread(words[:, e, u : u + 1], spread_words[:, e, u, :])
            nc.scalar.copy(out=gain[:].bitcast(F32), in_=spread_words[:].rearrange("q e u p -> q (e u p)"))

        pgrp = keep.tile([P, 2 * 4 * E * F], BF16, align_bytes=64, name="pgrp")
        pcode = keep.tile([P, 2 * E * F], U32, align_bytes=64, name="pcode")
        pscale = keep.tile([P, 2 * E * F], U8, align_bytes=64, name="pscale")
        ugrp = keep.tile([P, 4 * E * F], BF16, align_bytes=64, name="ugrp")
        ucode = keep.tile([P, E * F], U32, align_bytes=64, name="ucode")
        uscale = keep.tile([P, E * F], U8, align_bytes=64, name="uscale")

        def interleave(dst, sources, tag):
            laid = psum.tile([P, 1024], BF16, name=tag)
            for h in range(2):
                nc.tensor.matmul(laid[:, 512 * h : 512 * (h + 1)], lhsT=ident16[:], rhs=sources[h], start=True, stop=True)
            nc.scalar.copy(out=dst, in_=laid[:])

        def group_p(g):
            interleave(pgrp[:, 1024 * g : 1024 * (g + 1)], [praw[:, e, g].rearrange("q j f -> q f j") for e in range(E)], ("pp", "uu")[g])

        def group_u():
            interleave(ugrp[:], [uraw[:, e].rearrange("q j f -> q f j") for e in range(E)], "uu")

        def quant_p():
            nc.vector.quantize_mx(out=pcode[:].bitcast(X4), scales=pscale[:], in_=pgrp[:])

        def quant_u():
            nc.vector.quantize_mx(out=ucode[:].bitcast(X4), scales=uscale[:], in_=ugrp[:])

        xs, xw, xt, xg, xc, xsc = {}, {}, {}, {}, {}, {}
        acc, bb, bt, bg, bc, bsc = {}, {}, {}, {}, {}, {}
        pps, ups, sil, q, z, res = {}, {}, {}, {}, {}, {}
        sumsq = keep.tile([P, TILES * E], F32, name="sumsq")
        gate = keep.tile([P, TILES, E], F32, name="gate")

        def scale_x(n, start=0, stop=D):
            if start == 0:
                xs[n] = stage.tile([P, D], BF16, align_bytes=64, name="xs", bufs=5)
            nc.vector.tensor_tensor(out=xs[n][:, start:stop], in0=xb[n // 2][:, n % 2, start:stop].bitcast(F8), in1=xscale[:, start:stop], op=ALU.mult)

        def widen_x(n):
            xw[n] = stage.tile([P, D], BF16, name="xw", bufs=1)
            nc.scalar.copy(out=xw[n][:, WIDEN:D], in_=xb[n // 2][:, n % 2, WIDEN:D].bitcast(F8))

        def share_x(n):
            nc.vector.tensor_copy(out=xw[n][:, 0:WIDEN], in_=xb[n // 2][:, n % 2, 0:WIDEN].bitcast(F8))
            xs[n] = stage.tile([P, D], BF16, align_bytes=64, name="xs_apart", bufs=2)
            nc.gpsimd.tensor_tensor(
                out=xs[n][:].rearrange("q (u c e) -> q u c e", u=2, e=2),
                in0=xw[n][:].rearrange("q (c u e) -> q u c e", u=2, e=2),
                in1=xscale[:].rearrange("q (c u e) -> q u c e", u=2, e=2),
                op=ALU.mult,
            )

        def turn_x(n, tag="xt"):
            xt[n] = psum.tile([P, 2, 2, P], F32, name=tag)
            words = xs[n][:].bitcast(F32)
            for g in range(2):
                for u in range(2):
                    first = 256 * u + P * g
                    cols = slice(first, first + P) if n in xw else slice(256 * g + u, 256 * (g + 1), 2)
                    nc.tensor.transpose(xt[n][:, g, u, :], words[:, cols], ident[:])

        def leave_x(n):
            k, m = n // 2, n % 2
            if m == 0:
                xg[k] = stage.tile([P, 2 * D], BF16, align_bytes=64, name="xg", bufs=2)
            nc.scalar.copy(
                out=xg[k][:, D * m : D * (m + 1)].bitcast(F32).rearrange("q (g r u) -> q g r u", g=2, u=2),
                in_=xt[n][:].rearrange("q g u r -> q g r u"),
            )

        def quant_x(k):
            xc[k] = stage.tile([P, 4 * P], U32, align_bytes=64, name="xc", bufs=6)
            xsc[k] = stage.tile([P, 4 * P], U8, align_bytes=64, name="xsc", bufs=6)
            nc.vector.quantize_mx(out=xc[k][:].bitcast(X4), scales=xsc[k][:], in_=xg[k][:])

        def bank(tag):
            tile = psum.tile([P, 4 * F], F32, name=tag, bufs=4 if tag == "acc" else 1)
            return tile

        def mm_a(n, e):
            k, m = n // 2, n % 2
            if (n, e) not in acc:
                acc[n, e] = bank("acc")
            for g in range(2):
                cols = slice((2 * m + g) * P, (2 * m + g + 1) * P)
                nc.tensor.matmul_mx(
                    out=acc[n, e][:],
                    lhsT=xc[k][:, cols].bitcast(X4),
                    lhsT_scale=xsc[k][:, cols],
                    rhs=wcode[e, g][:].bitcast(X4),
                    rhs_scale=wscale[e, g][:],
                    start=(g == 0),
                    stop=(g == 1),
                )

        def square(n, e):
            junk = stage.tile([P, R], BF16, name="junk", bufs=2)
            nc.scalar.activation(out=junk[:], in_=acc[n, e][:], func=ACT.Square, accum_out=sumsq[:, 2 * n + e : 2 * n + e + 1])

        def gain_b(n, e):
            if e == 0:
                bb[n] = stage.tile([P, E * R], BF16, align_bytes=64, name="bb", bufs=3)
            cols = slice(e * R, (e + 1) * R)
            nc.vector.tensor_tensor(out=bb[n][:, cols], in0=acc[n, e][:], in1=gain[:, cols], op=ALU.mult)

        def turn_b(n, es=(0, 1), tag="bt"):
            bt[n, es] = psum.tile([P, E, 2, P], F32, name=tag)
            words = bb[n][:].bitcast(F32)
            for e in es:
                for u in range(2):
                    nc.tensor.transpose(bt[n, es][:, e, u, :], words[:, 256 * e + 128 * u : 256 * e + 128 * (u + 1)], ident[:])

        def leave_b(n, es=(0, 1)):
            k, first = n // 2, 2 * (n % 2) + es[0]
            if first == 0:
                bg[k] = stage.tile([P, 2 * E * R], BF16, align_bytes=64, name="bg", bufs=2)
            nc.scalar.copy(
                out=bg[k][:, R * first : R * (first + len(es))].bitcast(F32).rearrange("q (e r u) -> q e r u", e=len(es), u=2),
                in_=bt[n, es][:, es[0] : es[0] + len(es)].rearrange("q e u r -> q e r u"),
            )

        def quant_b(k, first=0, count=4):
            if first == 0:
                bc[k] = stage.tile([P, 4 * P], U32, align_bytes=64, name="bc", bufs=2)
                bsc[k] = stage.tile([P, 4 * P], U8, align_bytes=64, name="bsc", bufs=2)
            cols = slice(P * first, P * (first + count))
            nc.vector.quantize_mx(out=bc[k][:, cols].bitcast(X4), scales=bsc[k][:, cols], in_=bg[k][:, R * first : R * (first + count)])

        def mm_u(k, first=0, count=4, tag="uu"):
            ups[k, first] = bank(tag)
            for slot in range(first, first + count):
                cols = slice(slot * P, (slot + 1) * P)
                ecols = slice(slot % E * F, (slot % E + 1) * F)
                nc.tensor.matmul_mx(
                    out=ups[k, first][:, cols],
                    lhsT=bc[k][:, cols].bitcast(X4),
                    lhsT_scale=bsc[k][:, cols],
                    rhs=ucode[:, ecols].bitcast(X4),
                    rhs_scale=uscale[:, ecols],
                    start=True,
                    stop=True,
                )

        def mm_p(k, tag="pp"):
            pps[k] = bank(tag)
            for m in range(2):
                for g in range(2):
                    cols = slice((2 * m + g) * P, (2 * m + g + 1) * P)
                    gcols = slice(g * E * F, (g + 1) * E * F)
                    nc.tensor.matmul_mx(
                        out=pps[k][:, m * E * F : (m + 1) * E * F],
                        lhsT=xc[k][:, cols].bitcast(X4),
                        lhsT_scale=xsc[k][:, cols],
                        rhs=pcode[:, gcols].bitcast(X4),
                        rhs_scale=pscale[:, gcols],
                        start=(g == 0),
                        stop=(g == 1),
                    )

        def silu(k, first=0, count=4):
            cols = slice(F * first, F * (first + count))
            if first == 0:
                sil[k] = stage.tile([P, 4 * F], F32, name="sil", bufs=2)
            nc.scalar.activation(out=sil[k][:, cols], in_=ups[k, first][:, cols], func=ACT.Silu)

        def mix(k, first=0, count=4):
            cols = slice(F * first, F * (first + count))
            if first == 0:
                q[k] = stage.tile([P, 4 * F], F32, name="q", bufs=16)
            nc.vector.tensor_tensor(out=q[k][:, cols], in0=sil[k][:, cols], in1=pps[k][:, cols], op=ALU.mult)

        def weigh(n, on_scalar):
            k, m = n // 2, n % 2
            z[n] = stage.tile([P, F], F32, name="z", bufs=20)
            product = q[k][:, (2 * m + 1) * F : (2 * m + 2) * F]
            if on_scalar:
                nc.scalar.activation(out=z[n][:], in_=product, func=ACT.Copy, scale=gate[:, n, 1:2])
            else:
                nc.vector.tensor_scalar(out=z[n][:], in0=product, scalar1=gate[:, n, 1:2], scalar2=None, op0=ALU.mult)

        def store(k, ms):
            rows = out[256 * k : 256 * k + 256, :].rearrange("(p m) f -> p m f", m=2)
            nc.sync.dma_start(out=rows[:, ms], in_=res[k][:, ms])

        def join(n):
            k, m = n // 2, n % 2
            if m == 0:
                res[k] = stage.tile([P, 2, F], F32, name="res", bufs=8)
            nc.vector.scalar_tensor_tensor(
                out=res[k][:, m, :],
                in0=q[k][:, 2 * m * F : (2 * m + 1) * F],
                scalar=gate[:, n, 0:1],
                in1=z[n][:],
                op0=ALU.mult,
                op1=ALU.add,
            )
            if m == 1:
                store(k, slice(0, 2))

        def gate_steps(first, count):
            t0, nt = 2 * first, 2 * count
            ss = sumsq[:, E * t0 : E * (t0 + nt)]
            seed = stage.tile([P, E * nt], I32, name="seed", bufs=2)
            diff = stage.tile([P, nt], F32, name="diff", bufs=2)
            state = {"y": seed[:].bitcast(F32)}

            def start():
                nc.vector.tensor_scalar(out=seed[:], in0=ss.bitcast(I32), scalar1=0.5, scalar2=SQRT_SEED, op0=ALU.mult, op1=ALU.add)

            def recip():
                state["r"] = stage.tile([P, E * nt], F32, name="heron_r", bufs=2)
                nc.vector.reciprocal(out=state["r"][:], in_=state["y"])

            def divide():
                state["t"] = stage.tile([P, E * nt], F32, name="heron_t", bufs=2)
                nc.vector.scalar_tensor_tensor(out=state["t"][:], in0=ss, scalar=0.5, in1=state["r"][:], op0=ALU.mult, op1=ALU.mult)

            def average():
                y = stage.tile([P, E * nt], F32, name="heron_y", bufs=2)
                nc.vector.scalar_tensor_tensor(out=y[:], in0=state["y"], scalar=0.5, in1=state["t"][:], op0=ALU.mult, op1=ALU.add)
                state["y"] = y[:]

            def subtract():
                both = state["y"].rearrange("q (n e) -> q e n", e=E)
                nc.vector.tensor_tensor(out=diff[:], in0=both[:, 0], in1=both[:, 1], op=ALU.subtract)
                squashes.append(squash)

            def squash():
                h = stage.tile([P, nt], F32, name="tanh", bufs=2)
                nc.scalar.activation(out=h[:], in_=diff[:], func=ACT.Tanh, scale=0.5)
                for e in range(E):
                    nc.scalar.activation(out=gate[:, t0 : t0 + nt, e], in_=h[:], func=ACT.Copy, scale=(0.5, -0.5)[e], bias=0.5)
                gated.extend(range(t0, t0 + nt))

            return [start] + [recip, divide, average] * 3 + [subtract]

        def turn_pair(k):
            turn_x(2 * k)
            turn_x(2 * k + 1, "bt")
            leave_x(2 * k)
            leave_x(2 * k + 1)

        group_first_w()
        spread_gain()
        scale_x(0, 0, 512)
        scale_x(0, 512, D)
        scale_x(1)
        group_w(0, 1, nc.scalar.copy)
        turn_pair(0)
        quant_w(0, 0)
        group_w(1, 0, nc.vector.tensor_copy)
        quant_w(0, 1)
        quant_x(0)
        group_w(1, 1, nc.scalar.copy)
        group_u()
        for n in range(2):
            for e in range(E):
                acc[n, e] = bank("acc")
        for n in range(2):
            mm_a(n, 0)
        quant_w(1, 0)
        scale_x(2)
        square(0, 0)
        turn_x(2)
        leave_x(2)
        quant_w(1, 1)
        scale_x(3)
        for n in range(2):
            mm_a(n, 1)
        square(0, 1)
        widen_x(7)
        turn_x(3, "bt")
        leave_x(3)
        for e in range(E):
            square(1, e)
        group_p(0)
        scale_x(4)
        turn_x(4)
        leave_x(4)
        group_p(1)
        scale_x(5)
        scale_x(6)
        share_x(7)
        quant_x(1)

        small, fresh, squashes, gated, mixed, weighed = [], [], [], [], [], []
        ends, total = {}, 0
        for count in GROUPS:
            ends[2 * (total + count) - 1] = (total, count)
            total += count
        last = PAIRS - 1

        def weave():
            if small:
                small.pop(0)()

        def weigh_ready(count, on_scalar):
            for i in range(count):
                if gated and gated[0] in mixed:
                    weighed.append(gated[0])
                    weigh(gated.pop(0), on_scalar)

        for s in range(TILES - 1):
            pair = (s + SCALE_AHEAD) // 2 if s % 2 == 1 and s + SCALE_AHEAD < TILES else None
            before = weighed[:JOINS] if s < TILES - 2 else []
            weighed[:] = weighed[len(before) :]
            gain_b(s, 0)
            if s > TILES - SCALE_AHEAD:
                weave()
            gain_b(s, 1)
            if s > TILES - SCALE_AHEAD:
                weave()
            for e in (0, 1) if s % 2 == 1 else (1, 0) if s > 0 else ():
                square(s + 1, e)
            if pair:
                widen_x(2 * pair + 1)
            if s + 1 in ends:
                fresh.extend(gate_steps(*ends[s + 1]))
            if s % 2 == 0 and s >= 4:
                silu((s - 4) // 2)
            turns = [(turn_x, leave_x, s + TURN_AHEAD), (turn_b, leave_b, s - 1)]
            turns = [item for item in turns[:: 2 * (s % 2) - 1] if 0 <= item[2] < TILES]
            for turn, leave, n in turns:
                turn(n)
            for turn, leave, n in turns:
                leave(n)
            if squashes:
                squashes.pop(0)()
            elif s >= TILES - TURN_AHEAD:
                weigh_ready(3, True)
            if s == 1:
                quant_u()
            if s % 2 == 1 and s >= 5:
                mix((s - 5) // 2)
                mixed.extend((s - 5, s - 4))
                weave()
            if s % 2 == 1 and s >= 3:
                quant_b((s - 3) // 2)
                weave()
            if s + 2 < TILES:
                for e in range(E):
                    acc[s + 2, e] = bank("acc")
                for e in (1, 0) if s % 2 == 1 else (0, 1):
                    mm_a(s + 2, e)
            if s == 3:
                quant_p()
            if s % 2 == 1 and s >= 3:
                mm_u((s - 3) // 2)
                mm_p((s - 3) // 2)
            if s >= TILES - SCALE_AHEAD:
                for n in before:
                    join(n)
                if s < TILES - TURN_AHEAD:
                    weigh_ready(JOINS, False)
            if pair:
                scale_x(2 * pair)
                weave()
                share_x(2 * pair + 1)
            if s % 2 == 1 and (s + 3) // 2 < PAIRS:
                weave()
                quant_x((s + 3) // 2)
            small.extend(fresh)
            fresh.clear()

        def tick():
            weave()
            if squashes:
                squashes.pop()()
            else:
                weigh_ready(2, True)

        def fill():
            for m in weighed[:2]:
                join(m)
            weighed[:] = weighed[2:]
            tick()

        n = TILES - 1
        gain_b(n, 0)
        tick()
        turn_b(n - 1, tag="xt")
        leave_b(n - 1)
        mm_p(last - 1, "acc")
        gain_b(n, 1)
        tick()
        turn_b(n)
        leave_b(n)
        mm_p(last, "acc")
        fill()
        mix(last - 2)
        mixed.extend((n - 5, n - 4))
        tick()
        quant_b(last - 1)
        tick()
        mm_u(last - 1)
        quant_b(last, 0, 2)
        tick()
        quant_b(last, 2, 2)
        tick()
        mm_u(last, tag="acc")
        silu(last - 1)
        silu(last)
        while small:
            fill()
        mix(last - 1)
        mix(last)
        mixed.extend(range(n - 3, n + 1))
        weigh_ready(TILES, True)
        for m in weighed:
            join(m)
